import numpy as np
import ml_dtypes


def mxq(x, axis, fmt="e4m3"):
    dtype, down = {"e4m3": (ml_dtypes.float8_e4m3fn, 7), "e5m2": (ml_dtypes.float8_e5m2, 14)}[fmt]
    v = np.moveaxis(np.asarray(x, np.float32).astype(ml_dtypes.bfloat16).astype(np.float64), axis, -1)
    blocks = v.reshape(v.shape[:-1] + (-1, 32))
    amax = np.abs(blocks).max(-1, keepdims=True)
    byte = np.maximum(np.where(amax > 0, np.frexp(amax)[1] - 1 + 127, 0) - down, 1)
    scale = np.exp2(byte - 127.0)
    codes = (blocks / scale).astype(np.float32).astype(dtype).astype(np.float64)
    return np.moveaxis((codes * scale).reshape(v.shape), -1, axis)


WIDE = False


def mx_kscale(k):
    if not WIDE:
        return np.ones(k)
    levels = np.array([10, -10, 5, -5, 0])
    if k % 512:
        return np.exp2(np.random.permutation(np.resize(levels, k // 32))).repeat(32)
    a = np.empty((k // 512, 16))
    for p in range(k // 512):
        a[p, :8] = np.random.permutation(np.resize(levels, 8))
        for g in range(8):
            far = levels[np.abs(levels - a[p, g]) >= 10]
            a[p, g + 8] = far[np.random.randint(len(far))]
    return np.exp2(a.ravel()).repeat(32)


def f64(x):
    return np.asarray(x).astype(np.float64)


def striped(idx):
    return np.tile(idx.reshape(-1, 16).T, (8, 1)).astype(np.uint16)


def unstriped(offs):
    return offs[:16].T.reshape(-1).astype(np.int64)


E2M1 = np.array([0.0, 0.5, 1.0, 1.5, 2.0, 3.0, 4.0, 6.0, -0.0, -0.5, -1.0, -1.5, -2.0, -3.0, -4.0, -6.0])


def pack_weight(w, fmt):
    k, n = w.shape
    w = f64(np.asarray(w, np.float32).astype(ml_dtypes.bfloat16)).reshape(k // 32, 32, n)
    amax = np.abs(w).max(1)
    if fmt == "e4m3":
        byte = np.frexp(amax)[1] - 1 + 127 - 7
    else:
        mant, ex = np.frexp(amax / 6.0)
        byte = np.where(mant > 0.5, ex, ex - 1) + 127
    byte = np.clip(np.where(amax > 0, byte, 1), 1, 254)
    scaled = (w * np.exp2(127.0 - byte)[:, None, :]).reshape(k, n).astype(np.float32)
    by_word = np.ascontiguousarray(scaled.reshape(k // 512, 128, 4, n).transpose(0, 1, 3, 2))
    if fmt == "e4m3":
        words = by_word.astype(ml_dtypes.float8_e4m3fn).view(np.uint8)
    else:
        c = by_word.astype(ml_dtypes.float4_e2m1fn).view(np.uint8) & 0xF
        words = (c[..., 0::2] | (c[..., 1::2] << 4)).reshape(k // 512, 128, 2 * n)
    return np.ascontiguousarray(words), np.ascontiguousarray(byte.astype(np.uint8).reshape(k // 512, 16, n))


def unpack_weight(words, scales, fmt):
    g, _, n = scales.shape
    words = np.ascontiguousarray(words).reshape(g, 128, n, -1)
    if fmt == "e4m3":
        vals = words.view(ml_dtypes.float8_e4m3fn).astype(np.float64)
    else:
        nib = np.empty((g, 128, n, 4), np.uint8)
        nib[..., 0::2] = words & 0xF
        nib[..., 1::2] = words >> 4
        vals = E2M1[nib]
    vals = vals * np.repeat(np.exp2(scales.astype(np.float64) - 127.0), 8, axis=1)[..., None]
    return vals.transpose(0, 1, 3, 2).reshape(g * 512, n)


def silu(v):
    return v / (1.0 + np.exp(-np.maximum(v, -700.0)))


K, T, E, C, H, N = 1024, 512, 8, 128, 512, 128


def by_expert(wq, xq):
    return np.concatenate([wq[e].T @ xq[:, e * C:(e + 1) * C] for e in range(E)], axis=1)


def setup_inputs():
    n = np.random.standard_normal
    s = mx_kscale(K)
    u = mx_kscale(H)
    first = np.random.permutation(np.repeat(np.arange(E), T // E))
    second = (first + 1 + np.random.permutation(np.repeat(np.arange(E - 1), -(-T // (E - 1)))[:T])) % E
    while np.bincount(second, minlength=E).max() != T // E:
        load = np.bincount(second, minlength=E); hi, lo = int(load.argmax()), int(load.argmin())
        t = np.flatnonzero((second == hi) & (first != lo))[0]; second[t] = lo
    slot_token = np.empty(E * C, np.int64); pos = np.empty((2, T), np.int64); fill = np.zeros(E, np.int64)
    place = np.stack([np.random.permutation(C) for _ in range(E)])
    for r, deal in enumerate((first, second)):
        for t in np.random.permutation(T):
            e = deal[t]; j = e * C + place[e, fill[e]]; fill[e] += 1; slot_token[j] = t; pos[r, t] = j
    g = np.random.uniform(0.2, 0.8, T)
    partner = np.concatenate([np.random.permutation(T) for _ in range(-(-E * C // T))])[:E * C]
    x = pack_weight(n((K, T)) * s[:, None], "e4m3")
    w1 = [pack_weight(m, "e2m1") for m in n((E, K, H)) / np.sqrt(K) / s[None, :, None] * u]
    wp = [pack_weight(m, "e2m1") for m in n((E, K, H)) / np.sqrt(K) / s[None, :, None] * u]
    w2 = [pack_weight(m, "e2m1") for m in n((E, H, N)) / np.sqrt(H) / u[None, :, None]]
    return {
        "x_words": x[0],
        "x_scales": x[1],
        "w1_words": np.stack([m[0] for m in w1]),
        "w1_scales": np.stack([m[1] for m in w1]),
        "wp_words": np.stack([m[0] for m in wp]),
        "wp_scales": np.stack([m[1] for m in wp]),
        "w2_words": np.stack([m[0] for m in w2]),
        "w2_scales": np.stack([m[1] for m in w2]),
        "gate": np.stack([np.tile(g, (128, 1)), np.tile(1.0 - g, (128, 1))]).astype(np.float32),
        "offs": striped(slot_token),
        "pos1": striped(pos[0]),
        "pos2": striped(pos[1]),
        "offs2": striped(partner),
    }


def reference(x_words, x_scales, w1_words, w1_scales, wp_words, wp_scales, w2_words, w2_scales, gate, offs, pos1, pos2, offs2):
    w1 = np.stack([unpack_weight(w1_words[e], w1_scales[e], "e2m1") for e in range(E)])
    wp = np.stack([unpack_weight(wp_words[e], wp_scales[e], "e2m1") for e in range(E)])
    w2 = np.stack([unpack_weight(w2_words[e], w2_scales[e], "e2m1") for e in range(E)])
    idx, idx2 = unstriped(offs), unstriped(offs2)
    x = unpack_weight(x_words, x_scales, "e4m3")
    h = silu(by_expert(w1, x[:, idx]) + by_expert(wp, x[:, idx2]))
    y = by_expert(w2, mxq(h, 0, "e4m3"))
    out = sum(f64(gate[r, :1]) * y[:, unstriped(p)] for r, p in enumerate((pos1, pos2)))
    return out

@@ -1,0 +1,253 @@
+from contextlib import ExitStack
+
+import concourse.mybir as mybir
+from concourse.masks import make_identity
+
+K, T, E, C, H, N = 1024, 512, 8, 128, 512, 128
+FLOPS = 2 * E * C * (2 * K * H + H * N)
+
+F32 = mybir.dt.float32
+BF16 = mybir.dt.bfloat16
+I32 = mybir.dt.int32
+U32 = mybir.dt.uint32
+U16 = mybir.dt.uint16
+U8 = mybir.dt.uint8
+FP8X4 = mybir.dt.float8_e4m3fn_x4
+FP4X4 = mybir.dt.float4_e2m1fn_x4
+MULT = mybir.AluOpType.mult
+ADD = mybir.AluOpType.add
+SILU = mybir.ActivationFunctionType.Silu
+
+P = 128
+PASSES = K // 512
+SLOTS = E * C
+GROUP = 4
+WORD_RUNS = ((0, 1), (1, 3), (3, 4), (4, 5), (5, 7), (7, 8))
+SCALE_RUNS = ((0, 2), (2, 5), (5, 8))
+SCALE_STEP = (0, 1, 4)
+QUANT_RUNS = ((0, 4), (4, 6), (6, 7), (7, 8))
+Y_RUNS = ((0, 4), (4, 7), (7, 8))
+OUT_RUNS = ((0, 384), (384, 512))
+MOVED = 112
+
+
+def load_scale_rows(queue, plane, scales):
+    for r in range(4):
+        queue.dma_start(
+            out=plane[r:P:32, :, :].bitcast(I32),
+            in_=scales[:, r:16:4, :].rearrange("a q n -> q a n").bitcast(I32),
+        )
+
+
+def tile_moe_duo_silu_kernel(
+    tc, x_words, x_scales, w1_words, w1_scales, wp_words, wp_scales, w2_words, w2_scales,
+    gate, offs, pos1, pos2, offs2, out,
+):
+    nc = tc.nc
+    with ExitStack() as ctx:
+        keep = ctx.enter_context(tc.tile_pool(name="keep", bufs=1))
+        work = ctx.enter_context(tc.tile_pool(name="work", bufs=3))
+        pre_psum = ctx.enter_context(tc.psum_pool(name="pre_psum", bufs=3))
+        turn_psum = ctx.enter_context(tc.psum_pool(name="turn_psum", bufs=2))
+        y_psum = ctx.enter_context(tc.psum_pool(name="y_psum", bufs=1))
+
+        lists = [keep.tile([P, SLOTS // 16], U16, name=f"slot_list{a}") for a in range(2)]
+        back = [keep.tile([P, T // 16], U16, name=f"back_list{a}") for a in range(2)]
+        xw = keep.tile([P, PASSES, T], I32, align_bytes=64)
+        tok_scales = [
+            [keep.tile([P, 2, (e1 - e0) * C], U8, name=f"tok_scales{s}_{e0}", align_bytes=64) for e0, e1 in SCALE_RUNS]
+            for s in range(PASSES)
+        ]
+        xs = keep.tile([P, T], U8, align_bytes=64)
+        planes = [
+            [keep.tile([P, GROUP * PASSES, H], U8, name=f"plane{a}_{g}", align_bytes=64) for g in range(E // GROUP)]
+            for a in range(2)
+        ]
+        words = [
+            [keep.tile([P, 2 * PASSES, 2 * H], U8, name=f"words{a}_{c}", align_bytes=64) for c in range(E // 2)]
+            for a in range(2)
+        ]
+        w2_plane = keep.tile([P, E, N], U8, align_bytes=64)
+        w2w = keep.tile([P, E, 2 * N], U8, align_bytes=64)
+        gates = keep.tile([P, 2, T], F32)
+        ident = keep.tile([P, P], F32, align_bytes=64)
+        y = keep.tile([P, SLOTS], F32)
+
+        nc.gpsimd.memset(xs[:].bitcast(I32), 0)
+        for a in range(2):
+            nc.vector.memset(planes[a][0][:].bitcast(I32), 0)
+        for moved in tok_scales[1]:
+            nc.vector.memset(moved[:].bitcast(I32), 0)
+
+        w_words = (w1_words, wp_words)
+        w_scales = (w1_scales, wp_scales)
+
+        def load_words(a, c, queue=nc.sync):
+            queue.dma_start(
+                out=words[a][c][:].bitcast(I32),
+                in_=w_words[a][2 * c : 2 * c + 2].rearrange("e s p n -> p (e s) n").bitcast(I32),
+            )
+
+        def load_planes(a, g):
+            load_scale_rows(
+                nc.sync, planes[a][g], w_scales[a][GROUP * g : GROUP * (g + 1)].rearrange("e s b n -> (e s) b n")
+            )
+
+        nc.sync.dma_start(lists[0][:], offs)
+        for q in range(4):
+            nc.sync.dma_start(
+                out=xs[32 * q : 32 * q + 8, :].bitcast(I32), in_=x_scales[:, 4 * q : 4 * q + 4, :].bitcast(I32)
+            )
+        nc.sync.dma_start(out=xw[:], in_=x_words.rearrange("s p t d -> p s (t d)").bitcast(I32))
+        nc.sync.dma_start(lists[1][:], offs2)
+        load_words(0, 0)
+        load_planes(0, 0)
+        load_planes(1, 0)
+        load_words(1, 0, nc.gpsimd)
+        for a in range(2):
+            nc.gpsimd.memset(planes[a][1][:].bitcast(I32), 0)
+        make_identity(nc, ident[:])
+        nc.gpsimd.memset(w2_plane[:].bitcast(I32), 0)
+
+        def loads_behind(g):
+            if g == 0:
+                load_words(0, 1)
+                load_words(1, 1)
+            if g == 1:
+                load_planes(0, 1)
+                load_planes(1, 1)
+                load_words(0, 2)
+                load_words(1, 2)
+            if g == 2:
+                load_words(0, 3)
+                for e in (6, 7):
+                    nc.sync.dma_start(
+                        out=words[1][3][:, (e % 2) * PASSES : (e % 2 + 1) * PASSES, :].bitcast(I32),
+                        in_=wp_words[e].rearrange("s p n -> p s n").bitcast(I32),
+                    )
+                load_scale_rows(nc.sync, w2_plane, w2_scales.rearrange("e s b n -> (e s) b n"))
+                nc.sync.dma_start(
+                    out=w2w[:].bitcast(I32), in_=w2_words.rearrange("e s p n -> p (e s) n").bitcast(I32)
+                )
+                nc.sync.dma_start(back[0][:], pos1)
+                nc.sync.dma_start(back[1][:], pos2)
+                nc.sync.dma_start(out=gates[:], in_=gate.rearrange("r p t -> p r t"))
+
+        tok_words = {}
+        tok_planes = {}
+
+        def pass_order(e):
+            if e < 2:
+                return [(a, s) for s in range(PASSES) for a in range(2)]
+            return [(a, s) for a in range(2) for s in range(PASSES)]
+
+        def gather_scales(g):
+            e0, e1 = SCALE_RUNS[g]
+            for a in range(2):
+                nc.vector.tensor_copy(
+                    tok_scales[0][g][:, a, :], xs[:].indirect(lists[a][:, e0 * C // 16 : e1 * C // 16])
+                )
+            nc.sync.dma_start(
+                out=tok_scales[1][g][0:MOVED, :, :].bitcast(I32), in_=tok_scales[0][g][4 : 4 + MOVED, :, :].bitcast(I32)
+            )
+            loads_behind(g)
+            for e in range(e0, e1):
+                for a in range(2):
+                    for s in range(PASSES):
+                        tok_planes[a, s, e] = tok_scales[s][g][:, a, (e - e0) * C : (e - e0 + 1) * C]
+
+        def gather_words(e0, e1):
+            for a, s in pass_order(e0):
+                tile = keep.tile([P, (e1 - e0) * C], U32, name=f"tok_words{a}_{s}_{e0}", align_bytes=64)
+                nc.vector.tensor_copy(
+                    tile[:], xw[:, s, :].bitcast(U32).indirect(lists[a][:, e0 * C // 16 : e1 * C // 16])
+                )
+                for e in range(e0, e1):
+                    tok_words[a, s, e] = tile[:, (e - e0) * C : (e - e0 + 1) * C]
+
+        h = {}
+        grouped = keep.tile([P, E, 4 * C], BF16, align_bytes=64)
+        h_words = keep.tile([P, SLOTS], U32, align_bytes=64)
+        h_scales = keep.tile([P, SLOTS], U8, align_bytes=64)
+
+        def first_layer(e):
+            pre = pre_psum.tile([P, H], F32, name="pre")
+            for i, (a, s) in enumerate(pass_order(e)):
+                nc.tensor.matmul_mx(
+                    out=pre[:],
+                    lhsT=tok_words[a, s, e].bitcast(FP8X4),
+                    lhsT_scale=tok_planes[a, s, e],
+                    rhs=words[a][e // 2][:, (e % 2) * PASSES + s, :].bitcast(FP4X4),
+                    rhs_scale=planes[a][e // GROUP][:, (e % GROUP) * PASSES + s, :],
+                    start=(i == 0),
+                    stop=(i == 2 * PASSES - 1),
+                )
+            h[e] = work.tile([P, H], BF16, name="h", align_bytes=64)
+            nc.scalar.activation(
+                h[e][:].rearrange("c (u p d) -> c u p d", u=2, d=2),
+                pre[:].rearrange("c (p u d) -> c u p d", u=2, d=2),
+                SILU,
+            )
+
+        def turn(e):
+            turned = turn_psum.tile([P, 2, C], F32, name="turned")
+            for u in range(2):
+                nc.tensor.transpose(turned[:, u, :], h[e][:].bitcast(F32)[:, u * P : (u + 1) * P], ident[:])
+            nc.scalar.copy(
+                grouped[:, e, :].bitcast(F32).rearrange("p (c u) -> p c u", u=2),
+                turned[:].rearrange("p u c -> p c u"),
+            )
+
+        for step in range(E + 1):
+            for g in range(len(SCALE_RUNS)):
+                if step == SCALE_STEP[g]:
+                    gather_scales(g)
+            for e0, e1 in WORD_RUNS:
+                if step == e0:
+                    gather_words(e0, e1)
+            if step < E:
+                first_layer(step)
+            if step >= 1:
+                turn(step - 1)
+
+        for e0, e1 in QUANT_RUNS:
+            nc.vector.quantize_mx(
+                out=h_words[:, e0 * C : e1 * C].bitcast(FP8X4),
+                scales=h_scales[:, e0 * C : e1 * C],
+                in_=grouped[:, e0:e1, :].rearrange("p e c -> p (e c)"),
+            )
+        for e0, e1 in Y_RUNS:
+            acc = y_psum.tile([P, (e1 - e0) * C], F32, name=f"acc{e0}")
+            for e in range(e0, e1):
+                nc.tensor.matmul_mx(
+                    out=acc[:, (e - e0) * C : (e - e0 + 1) * C],
+                    lhsT=w2w[:, e, :].bitcast(FP4X4),
+                    lhsT_scale=w2_plane[:, e, :],
+                    rhs=h_words[:, e * C : (e + 1) * C].bitcast(FP8X4),
+                    rhs_scale=h_scales[:, e * C : (e + 1) * C],
+                    start=True,
+                    stop=True,
+                )
+            if e0 == 0:
+                nc.vector.tensor_copy(y[:, e0 * C : e1 * C], acc[:])
+            else:
+                nc.scalar.copy(y[:, e0 * C : e1 * C], acc[:])
+
+        parts = [keep.tile([P, T], F32, name=f"part{r}") for r in range(2)]
+        result = keep.tile([P, T], F32)
+
+        def fetch(r, t0, t1):
+            nc.vector.tensor_tensor(
+                parts[r][:, t0:t1], y[:].indirect(back[r][:, t0 // 16 : t1 // 16]), gates[:, r, t0:t1], MULT
+            )
+
+        def finish(t0, t1):
+            nc.vector.tensor_tensor(result[:, t0:t1], parts[0][:, t0:t1], parts[1][:, t0:t1], ADD)
+            nc.sync.dma_start(out=out[:, t0:t1], in_=result[:, t0:t1])
+
+        fetch(0, *OUT_RUNS[0])
+        fetch(1, *OUT_RUNS[0])
+        fetch(0, *OUT_RUNS[1])
+        finish(*OUT_RUNS[0])
+        fetch(1, *OUT_RUNS[1])
+        finish(*OUT_RUNS[1])

@@ -21,10 +21,12 @@ SILU = mybir.ActivationFunctionType.Silu
 P = 128
 PASSES = K // 512
 SLOTS = E * C
-GROUP = 4
-WORD_RUNS = ((0, 1), (1, 3), (3, 4), (4, 5), (5, 7), (7, 8))
-SCALE_RUNS = ((0, 2), (2, 5), (5, 8))
-SCALE_STEP = (0, 1, 4)
+PLANE_RUNS = ((0, 5), (5, 8))
+LOAD_RUNS = ((0, 1), (1, 3), (3, 5), (5, 6), (6, 7), (7, 8))
+CHUNK = 256
+WORD_RUNS = ((0, 1), (1, 2), (2, 3), (3, 5), (5, 7), (7, 8))
+SCALE_RUNS = ((0, 4), (4, 8))
+SCALE_STEP = (0, 2)
 QUANT_RUNS = ((0, 4), (4, 6), (6, 7), (7, 8))
 Y_RUNS = ((0, 4), (4, 7), (7, 8))
 OUT_RUNS = ((0, 384), (384, 512))
@@ -46,10 +48,9 @@ def tile_moe_duo_silu_kernel(
     nc = tc.nc
     with ExitStack() as ctx:
         keep = ctx.enter_context(tc.tile_pool(name="keep", bufs=1))
-        work = ctx.enter_context(tc.tile_pool(name="work", bufs=3))
-        pre_psum = ctx.enter_context(tc.psum_pool(name="pre_psum", bufs=3))
+        work = ctx.enter_context(tc.tile_pool(name="work", bufs=4))
+        pre_psum = ctx.enter_context(tc.psum_pool(name="pre_psum", bufs=6))
         turn_psum = ctx.enter_context(tc.psum_pool(name="turn_psum", bufs=2))
-        y_psum = ctx.enter_context(tc.psum_pool(name="y_psum", bufs=1))
 
         lists = [keep.tile([P, SLOTS // 16], U16, name=f"slot_list{a}") for a in range(2)]
         back = [keep.tile([P, T // 16], U16, name=f"back_list{a}") for a in range(2)]
@@ -60,11 +61,11 @@ def tile_moe_duo_silu_kernel(
         ]
         xs = keep.tile([P, T], U8, align_bytes=64)
         planes = [
-            [keep.tile([P, GROUP * PASSES, H], U8, name=f"plane{a}_{g}", align_bytes=64) for g in range(E // GROUP)]
+            [keep.tile([P, (e1 - e0) * PASSES, H], U8, name=f"plane{a}_{e0}", align_bytes=64) for e0, e1 in PLANE_RUNS]
             for a in range(2)
         ]
         words = [
-            [keep.tile([P, 2 * PASSES, 2 * H], U8, name=f"words{a}_{c}", align_bytes=64) for c in range(E // 2)]
+            [keep.tile([P, (e1 - e0) * PASSES, 2 * H], U8, name=f"words{a}_{e0}", align_bytes=64) for e0, e1 in LOAD_RUNS]
             for a in range(2)
         ]
         w2_plane = keep.tile([P, E, N], U8, align_bytes=64)
@@ -74,57 +75,53 @@ def tile_moe_duo_silu_kernel(
         y = keep.tile([P, SLOTS], F32)
 
         nc.gpsimd.memset(xs[:].bitcast(I32), 0)
+        make_identity(nc, ident[:])
         for a in range(2):
             nc.vector.memset(planes[a][0][:].bitcast(I32), 0)
         for moved in tok_scales[1]:
             nc.vector.memset(moved[:].bitcast(I32), 0)
+        for a in range(2):
+            nc.vector.memset(planes[a][1][:].bitcast(I32), 0)
+        nc.vector.memset(w2_plane[:].bitcast(I32), 0)
 
         w_words = (w1_words, wp_words)
         w_scales = (w1_scales, wp_scales)
 
-        def load_words(a, c, queue=nc.sync):
-            queue.dma_start(
+        def load_words(a, c):
+            e0, e1 = LOAD_RUNS[c]
+            nc.sync.dma_start(
                 out=words[a][c][:].bitcast(I32),
-                in_=w_words[a][2 * c : 2 * c + 2].rearrange("e s p n -> p (e s) n").bitcast(I32),
+                in_=w_words[a][e0:e1].rearrange("e s p n -> p (e s) n").bitcast(I32),
             )
 
         def load_planes(a, g):
-            load_scale_rows(
-                nc.sync, planes[a][g], w_scales[a][GROUP * g : GROUP * (g + 1)].rearrange("e s b n -> (e s) b n")
-            )
+            e0, e1 = PLANE_RUNS[g]
+            load_scale_rows(nc.sync, planes[a][g], w_scales[a][e0:e1].rearrange("e s b n -> (e s) b n"))
 
-        nc.sync.dma_start(lists[0][:], offs)
         for q in range(4):
             nc.sync.dma_start(
                 out=xs[32 * q : 32 * q + 8, :].bitcast(I32), in_=x_scales[:, 4 * q : 4 * q + 4, :].bitcast(I32)
             )
         nc.sync.dma_start(out=xw[:], in_=x_words.rearrange("s p t d -> p s (t d)").bitcast(I32))
+        nc.sync.dma_start(lists[0][:], offs)
         nc.sync.dma_start(lists[1][:], offs2)
-        load_words(0, 0)
+
+        def load_experts(c0, c1):
+            for c in range(c0, c1):
+                load_words(0, c)
+                load_words(1, c)
+
+        load_experts(0, 1)
         load_planes(0, 0)
         load_planes(1, 0)
-        load_words(1, 0, nc.gpsimd)
-        for a in range(2):
-            nc.gpsimd.memset(planes[a][1][:].bitcast(I32), 0)
-        make_identity(nc, ident[:])
-        nc.gpsimd.memset(w2_plane[:].bitcast(I32), 0)
 
         def loads_behind(g):
             if g == 0:
-                load_words(0, 1)
-                load_words(1, 1)
+                load_experts(1, 3)
             if g == 1:
                 load_planes(0, 1)
                 load_planes(1, 1)
-                load_words(0, 2)
-                load_words(1, 2)
-            if g == 2:
-                load_words(0, 3)
-                for e in (6, 7):
-                    nc.sync.dma_start(
-                        out=words[1][3][:, (e % 2) * PASSES : (e % 2 + 1) * PASSES, :].bitcast(I32),
-                        in_=wp_words[e].rearrange("s p n -> p s n").bitcast(I32),
-                    )
+                load_experts(3, 6)
                 load_scale_rows(nc.sync, w2_plane, w2_scales.rearrange("e s b n -> (e s) b n"))
                 nc.sync.dma_start(
                     out=w2w[:].bitcast(I32), in_=w2_words.rearrange("e s p n -> p (e s) n").bitcast(I32)
@@ -144,9 +141,11 @@ def tile_moe_duo_silu_kernel(
         def gather_scales(g):
             e0, e1 = SCALE_RUNS[g]
             for a in range(2):
-                nc.vector.tensor_copy(
-                    tok_scales[0][g][:, a, :], xs[:].indirect(lists[a][:, e0 * C // 16 : e1 * C // 16])
-                )
+                for j in range(e0 * C, e1 * C, CHUNK):
+                    nc.vector.tensor_copy(
+                        tok_scales[0][g][:, a, j - e0 * C : j - e0 * C + CHUNK],
+                        xs[:].indirect(lists[a][:, j // 16 : (j + CHUNK) // 16]),
+                    )
             nc.sync.dma_start(
                 out=tok_scales[1][g][0:MOVED, :, :].bitcast(I32), in_=tok_scales[0][g][4 : 4 + MOVED, :, :].bitcast(I32)
             )
@@ -171,14 +170,16 @@ def tile_moe_duo_silu_kernel(
         h_scales = keep.tile([P, SLOTS], U8, align_bytes=64)
 
         def first_layer(e):
+            g = [e0 <= e < e1 for e0, e1 in PLANE_RUNS].index(True)
+            c = [e0 <= e < e1 for e0, e1 in LOAD_RUNS].index(True)
             pre = pre_psum.tile([P, H], F32, name="pre")
             for i, (a, s) in enumerate(pass_order(e)):
                 nc.tensor.matmul_mx(
                     out=pre[:],
                     lhsT=tok_words[a, s, e].bitcast(FP8X4),
                     lhsT_scale=tok_planes[a, s, e],
-                    rhs=words[a][e // 2][:, (e % 2) * PASSES + s, :].bitcast(FP4X4),
-                    rhs_scale=planes[a][e // GROUP][:, (e % GROUP) * PASSES + s, :],
+                    rhs=words[a][c][:, (e - LOAD_RUNS[c][0]) * PASSES + s, :].bitcast(FP4X4),
+                    rhs_scale=planes[a][g][:, (e - PLANE_RUNS[g][0]) * PASSES + s, :],
                     start=(i == 0),
                     stop=(i == 2 * PASSES - 1),
                 )
@@ -217,7 +218,7 @@ def tile_moe_duo_silu_kernel(
                 in_=grouped[:, e0:e1, :].rearrange("p e c -> p (e c)"),
             )
         for e0, e1 in Y_RUNS:
-            acc = y_psum.tile([P, (e1 - e0) * C], F32, name=f"acc{e0}")
+            acc = pre_psum.tile([P, (e1 - e0) * C], F32, name="pre")
             for e in range(e0, e1):
                 nc.tensor.matmul_mx(
                     out=acc[:, (e - e0) * C : (e - e0 + 1) * C],

@@ -23,10 +23,9 @@ PASSES = K // 512
 SLOTS = E * C
 PLANE_RUNS = ((0, 5), (5, 8))
 LOAD_RUNS = ((0, 1), (1, 3), (3, 5), (5, 6), (6, 7), (7, 8))
-CHUNK = 256
-WORD_RUNS = ((0, 1), (1, 2), (2, 3), (3, 5), (5, 7), (7, 8))
-SCALE_RUNS = ((0, 4), (4, 8))
-SCALE_STEP = (0, 2)
+CHUNK = 384
+SCALE_RUNS = ((0, 3), (3, 8))
+SCALE_STEP = (0, 1)
 QUANT_RUNS = ((0, 4), (4, 6), (6, 7), (7, 8))
 Y_RUNS = ((0, 4), (4, 7), (7, 8))
 OUT_RUNS = ((0, 384), (384, 512))
@@ -98,13 +97,13 @@ def tile_moe_duo_silu_kernel(
             e0, e1 = PLANE_RUNS[g]
             load_scale_rows(nc.sync, planes[a][g], w_scales[a][e0:e1].rearrange("e s b n -> (e s) b n"))
 
+        nc.sync.dma_start(lists[0][:], offs)
+        nc.sync.dma_start(lists[1][:], offs2)
         for q in range(4):
-            nc.sync.dma_start(
+            nc.scalar.dma_start(
                 out=xs[32 * q : 32 * q + 8, :].bitcast(I32), in_=x_scales[:, 4 * q : 4 * q + 4, :].bitcast(I32)
             )
         nc.sync.dma_start(out=xw[:], in_=x_words.rearrange("s p t d -> p s (t d)").bitcast(I32))
-        nc.sync.dma_start(lists[0][:], offs)
-        nc.sync.dma_start(lists[1][:], offs2)
 
         def load_experts(c0, c1):
             for c in range(c0, c1):
@@ -122,29 +121,30 @@ def tile_moe_duo_silu_kernel(
                 load_planes(0, 1)
                 load_planes(1, 1)
                 load_experts(3, 6)
-                load_scale_rows(nc.sync, w2_plane, w2_scales.rearrange("e s b n -> (e s) b n"))
                 nc.sync.dma_start(
                     out=w2w[:].bitcast(I32), in_=w2_words.rearrange("e s p n -> p (e s) n").bitcast(I32)
                 )
+                load_scale_rows(nc.sync, w2_plane, w2_scales.rearrange("e s b n -> (e s) b n"))
+                nc.sync.dma_start(out=gates[:], in_=gate.rearrange("r p t -> p r t"))
                 nc.sync.dma_start(back[0][:], pos1)
                 nc.sync.dma_start(back[1][:], pos2)
-                nc.sync.dma_start(out=gates[:], in_=gate.rearrange("r p t -> p r t"))
 
         tok_words = {}
         tok_planes = {}
 
         def pass_order(e):
-            if e < 2:
+            if e == 0:
                 return [(a, s) for s in range(PASSES) for a in range(2)]
             return [(a, s) for a in range(2) for s in range(PASSES)]
 
         def gather_scales(g):
             e0, e1 = SCALE_RUNS[g]
             for a in range(2):
-                for j in range(e0 * C, e1 * C, CHUNK):
+                for j0 in range(e0 * C, e1 * C, CHUNK):
+                    j1 = min(j0 + CHUNK, e1 * C)
                     nc.vector.tensor_copy(
-                        tok_scales[0][g][:, a, j - e0 * C : j - e0 * C + CHUNK],
-                        xs[:].indirect(lists[a][:, j // 16 : (j + CHUNK) // 16]),
+                        tok_scales[0][g][:, a, j0 - e0 * C : j1 - e0 * C],
+                        xs[:].indirect(lists[a][:, j0 // 16 : j1 // 16]),
                     )
             nc.sync.dma_start(
                 out=tok_scales[1][g][0:MOVED, :, :].bitcast(I32), in_=tok_scales[0][g][4 : 4 + MOVED, :, :].bitcast(I32)
@@ -203,7 +203,7 @@ def tile_moe_duo_silu_kernel(
             for g in range(len(SCALE_RUNS)):
                 if step == SCALE_STEP[g]:
                     gather_scales(g)
-            for e0, e1 in WORD_RUNS:
+            for e0, e1 in LOAD_RUNS:
                 if step == e0:
                     gather_words(e0, e1)
             if step < E:

@@ -21,15 +21,15 @@ SILU = mybir.ActivationFunctionType.Silu
 P = 128
 PASSES = K // 512
 SLOTS = E * C
-PLANE_RUNS = ((0, 5), (5, 8))
-LOAD_RUNS = ((0, 1), (1, 3), (3, 5), (5, 6), (6, 7), (7, 8))
-CHUNK = 384
-SCALE_RUNS = ((0, 3), (3, 8))
-SCALE_STEP = (0, 1)
+GROUPS = ((0, 3), (3, 6), (6, 8))
 QUANT_RUNS = ((0, 4), (4, 6), (6, 7), (7, 8))
 Y_RUNS = ((0, 4), (4, 7), (7, 8))
 OUT_RUNS = ((0, 384), (384, 512))
 MOVED = 112
+RING = 2
+TOKEN_GROUPS = ((0, 2), (2, 5), (5, 8))
+TURNS = ((0, 2), (2, 4), (4, 6), (6, 7), (7, 8))
+HELD = (1, 3, 5, 6)
 
 
 def load_scale_rows(queue, plane, scales):
@@ -47,27 +47,24 @@ def tile_moe_duo_silu_kernel(
     nc = tc.nc
     with ExitStack() as ctx:
         keep = ctx.enter_context(tc.tile_pool(name="keep", bufs=1))
-        work = ctx.enter_context(tc.tile_pool(name="work", bufs=4))
         pre_psum = ctx.enter_context(tc.psum_pool(name="pre_psum", bufs=6))
         turn_psum = ctx.enter_context(tc.psum_pool(name="turn_psum", bufs=2))
 
         lists = [keep.tile([P, SLOTS // 16], U16, name=f"slot_list{a}") for a in range(2)]
         back = [keep.tile([P, T // 16], U16, name=f"back_list{a}") for a in range(2)]
         xw = keep.tile([P, PASSES, T], I32, align_bytes=64)
-        tok_scales = [
-            [keep.tile([P, 2, (e1 - e0) * C], U8, name=f"tok_scales{s}_{e0}", align_bytes=64) for e0, e1 in SCALE_RUNS]
-            for s in range(PASSES)
-        ]
+        gathered = [keep.tile([P, 2 * (e1 - e0) * C], U8, name=f"gathered{e0}", align_bytes=64) for e0, e1 in TOKEN_GROUPS]
+        moved = [keep.tile([P, 2 * 3 * C], U8, name=f"moved{g}", align_bytes=64) for g in range(RING)]
         xs = keep.tile([P, T], U8, align_bytes=64)
         planes = [
-            [keep.tile([P, (e1 - e0) * PASSES, H], U8, name=f"plane{a}_{e0}", align_bytes=64) for e0, e1 in PLANE_RUNS]
+            [keep.tile([P, (e1 - e0) * PASSES, H], U8, name=f"plane{a}_{e0}", align_bytes=64) for e0, e1 in GROUPS[:RING]]
             for a in range(2)
         ]
         words = [
-            [keep.tile([P, (e1 - e0) * PASSES, 2 * H], U8, name=f"words{a}_{e0}", align_bytes=64) for e0, e1 in LOAD_RUNS]
+            [keep.tile([P, PASSES, 2 * H], U8, name=f"words{a}_{e}", align_bytes=64) for e in range(E)]
             for a in range(2)
         ]
-        w2_plane = keep.tile([P, E, N], U8, align_bytes=64)
+        w2_plane = planes[0][1][:, 0:PASSES, :].rearrange("p s (q n) -> p (s q) n", n=N)
         w2w = keep.tile([P, E, 2 * N], U8, align_bytes=64)
         gates = keep.tile([P, 2, T], F32)
         ident = keep.tile([P, P], F32, align_bytes=64)
@@ -75,27 +72,24 @@ def tile_moe_duo_silu_kernel(
 
         nc.gpsimd.memset(xs[:].bitcast(I32), 0)
         make_identity(nc, ident[:])
-        for a in range(2):
-            nc.vector.memset(planes[a][0][:].bitcast(I32), 0)
-        for moved in tok_scales[1]:
-            nc.vector.memset(moved[:].bitcast(I32), 0)
-        for a in range(2):
-            nc.vector.memset(planes[a][1][:].bitcast(I32), 0)
-        nc.vector.memset(w2_plane[:].bitcast(I32), 0)
+        for g in range(RING):
+            for a in range(2):
+                nc.vector.memset(planes[a][g][:].bitcast(I32), 0)
+        for g in range(RING):
+            nc.vector.memset(moved[g][:].bitcast(I32), 0)
 
         w_words = (w1_words, wp_words)
         w_scales = (w1_scales, wp_scales)
 
-        def load_words(a, c):
-            e0, e1 = LOAD_RUNS[c]
+        def load_words(a, e):
             nc.sync.dma_start(
-                out=words[a][c][:].bitcast(I32),
-                in_=w_words[a][e0:e1].rearrange("e s p n -> p (e s) n").bitcast(I32),
+                out=words[a][e][:].bitcast(I32),
+                in_=w_words[a][e].rearrange("s p n -> p s n").bitcast(I32),
             )
 
         def load_planes(a, g):
-            e0, e1 = PLANE_RUNS[g]
-            load_scale_rows(nc.sync, planes[a][g], w_scales[a][e0:e1].rearrange("e s b n -> (e s) b n"))
+            e0, e1 = GROUPS[g]
+            load_scale_rows(nc.sync, planes[a][g % RING][:, 0 : (e1 - e0) * PASSES, :], w_scales[a][e0:e1].rearrange("e s b n -> (e s) b n"))
 
         nc.sync.dma_start(lists[0][:], offs)
         nc.sync.dma_start(lists[1][:], offs2)
@@ -105,29 +99,25 @@ def tile_moe_duo_silu_kernel(
             )
         nc.sync.dma_start(out=xw[:], in_=x_words.rearrange("s p t d -> p s (t d)").bitcast(I32))
 
-        def load_experts(c0, c1):
-            for c in range(c0, c1):
-                load_words(0, c)
-                load_words(1, c)
+        def load_group(g):
+            e0, e1 = GROUPS[g]
+            for a in range(2):
+                if g == 0 and a == 0:
+                    load_words(a, e0)
+                    load_planes(a, g)
+                else:
+                    load_planes(a, g)
+                    load_words(a, e0)
+            for e in range(e0 + 1, e1):
+                for a in range(2):
+                    load_words(a, e)
 
-        load_experts(0, 1)
-        load_planes(0, 0)
-        load_planes(1, 0)
-
-        def loads_behind(g):
-            if g == 0:
-                load_experts(1, 3)
-            if g == 1:
-                load_planes(0, 1)
-                load_planes(1, 1)
-                load_experts(3, 6)
-                nc.sync.dma_start(
-                    out=w2w[:].bitcast(I32), in_=w2_words.rearrange("e s p n -> p (e s) n").bitcast(I32)
-                )
-                load_scale_rows(nc.sync, w2_plane, w2_scales.rearrange("e s b n -> (e s) b n"))
-                nc.sync.dma_start(out=gates[:], in_=gate.rearrange("r p t -> p r t"))
-                nc.sync.dma_start(back[0][:], pos1)
-                nc.sync.dma_start(back[1][:], pos2)
+        def load_last():
+            load_scale_rows(nc.sync, w2_plane, w2_scales.rearrange("e s b n -> (e s) b n"))
+            nc.sync.dma_start(out=w2w[:].bitcast(I32), in_=w2_words.rearrange("e s p n -> p (e s) n").bitcast(I32))
+            nc.sync.dma_start(back[0][:], pos1)
+            nc.sync.dma_start(back[1][:], pos2)
+            nc.sync.dma_start(out=gates[:], in_=gate.rearrange("r p t -> p r t"))
 
         tok_words = {}
         tok_planes = {}
@@ -138,78 +128,94 @@ def tile_moe_duo_silu_kernel(
             return [(a, s) for a in range(2) for s in range(PASSES)]
 
         def gather_scales(g):
-            e0, e1 = SCALE_RUNS[g]
+            e0, e1 = TOKEN_GROUPS[g]
+            width = (e1 - e0) * C
             for a in range(2):
-                for j0 in range(e0 * C, e1 * C, CHUNK):
-                    j1 = min(j0 + CHUNK, e1 * C)
-                    nc.vector.tensor_copy(
-                        tok_scales[0][g][:, a, j0 - e0 * C : j1 - e0 * C],
-                        xs[:].indirect(lists[a][:, j0 // 16 : j1 // 16]),
-                    )
-            nc.sync.dma_start(
-                out=tok_scales[1][g][0:MOVED, :, :].bitcast(I32), in_=tok_scales[0][g][4 : 4 + MOVED, :, :].bitcast(I32)
+                nc.vector.tensor_copy(
+                    gathered[g][:, a * width : (a + 1) * width], xs[:].indirect(lists[a][:, e0 * C // 16 : e1 * C // 16])
+                )
+            queue = nc.gpsimd if g == 0 else nc.gpsimd
+            queue.dma_start(
+                out=moved[g % RING][0:MOVED, 0 : 2 * width].bitcast(I32), in_=gathered[g][4 : 4 + MOVED, :].bitcast(I32)
             )
-            loads_behind(g)
             for e in range(e0, e1):
                 for a in range(2):
-                    for s in range(PASSES):
-                        tok_planes[a, s, e] = tok_scales[s][g][:, a, (e - e0) * C : (e - e0 + 1) * C]
+                    j = a * width + (e - e0) * C
+                    tok_planes[a, 0, e] = gathered[g][:, j : j + C]
+                    tok_planes[a, 1, e] = moved[g % RING][:, j : j + C]
 
-        def gather_words(e0, e1):
-            for a, s in pass_order(e0):
-                tile = keep.tile([P, (e1 - e0) * C], U32, name=f"tok_words{a}_{s}_{e0}", align_bytes=64)
+        def gather_words(e):
+            for a, s in pass_order(e):
+                tile = keep.tile([P, C], U32, name=f"tok_words{a}_{s}_{e}", tag=f"tok{a}_{s}_{e}", align_bytes=64)
                 nc.vector.tensor_copy(
-                    tile[:], xw[:, s, :].bitcast(U32).indirect(lists[a][:, e0 * C // 16 : e1 * C // 16])
+                    tile[:], xw[:, s, :].bitcast(U32).indirect(lists[a][:, e * C // 16 : (e + 1) * C // 16])
                 )
-                for e in range(e0, e1):
-                    tok_words[a, s, e] = tile[:, (e - e0) * C : (e - e0 + 1) * C]
+                tok_words[a, s, e] = tile[:]
 
-        h = {}
+        pre = {}
         grouped = keep.tile([P, E, 4 * C], BF16, align_bytes=64)
         h_words = keep.tile([P, SLOTS], U32, align_bytes=64)
         h_scales = keep.tile([P, SLOTS], U8, align_bytes=64)
 
         def first_layer(e):
-            g = [e0 <= e < e1 for e0, e1 in PLANE_RUNS].index(True)
-            c = [e0 <= e < e1 for e0, e1 in LOAD_RUNS].index(True)
-            pre = pre_psum.tile([P, H], F32, name="pre")
+            g = [e0 <= e < e1 for e0, e1 in GROUPS].index(True)
+            pre[e] = pre_psum.tile([P, H], F32, name="pre")
             for i, (a, s) in enumerate(pass_order(e)):
                 nc.tensor.matmul_mx(
-                    out=pre[:],
+                    out=pre[e][:],
                     lhsT=tok_words[a, s, e].bitcast(FP8X4),
                     lhsT_scale=tok_planes[a, s, e],
-                    rhs=words[a][c][:, (e - LOAD_RUNS[c][0]) * PASSES + s, :].bitcast(FP4X4),
-                    rhs_scale=planes[a][g][:, (e - PLANE_RUNS[g][0]) * PASSES + s, :],
+                    rhs=words[a][e][:, s, :].bitcast(FP4X4),
+                    rhs_scale=planes[a][g % RING][:, (e - GROUPS[g][0]) * PASSES + s, :],
                     start=(i == 0),
                     stop=(i == 2 * PASSES - 1),
                 )
-            h[e] = work.tile([P, H], BF16, name="h", align_bytes=64)
-            nc.scalar.activation(
-                h[e][:].rearrange("c (u p d) -> c u p d", u=2, d=2),
-                pre[:].rearrange("c (p u d) -> c u p d", u=2, d=2),
-                SILU,
+
+        h = {}
+
+        def silu(e):
+            sums = pre[e][:].rearrange("c (p u d) -> c u p d", u=2, d=2)
+            if e in HELD or e == E - 1:
+                for u in range(2):
+                    tag = f"tok0_0_{e + 1}" if u == 1 else f"h{e}"
+                    half = keep.tile([P, H // 2], BF16, name=f"h{e}_{u}", tag=tag, align_bytes=64)
+                    nc.scalar.activation(half[:].rearrange("c (p d) -> c p d", d=2), sums[:, u, :, :], SILU)
+                    h[e, u] = half[:].bitcast(F32)
+            else:
+                both = keep.tile([P, H], BF16, name=f"h{e}", align_bytes=64)
+                nc.scalar.activation(both[:].rearrange("c (u p d) -> c u p d", u=2, d=2), sums, SILU)
+                for u in range(2):
+                    h[e, u] = both[:].bitcast(F32)[:, u * P : (u + 1) * P]
+
+        def turn(e0, e1):
+            turned = turn_psum.tile([P, e1 - e0, 2, C], F32, name="turned")
+            order = [(e, u) for e in range(e0, e1) for u in range(2)]
+            for e, u in (order if e0 == E - 1 else reversed(order)):
+                nc.tensor.transpose(turned[:, e - e0, u, :], h[e, u], ident[:])
+            copy = nc.vector.tensor_copy if e0 == E - 2 else nc.scalar.copy
+            copy(
+                grouped[:, e0:e1, :].bitcast(F32).rearrange("p e (c u) -> p e c u", u=2),
+                turned[:].rearrange("p e u c -> p e c u"),
             )
 
-        def turn(e):
-            turned = turn_psum.tile([P, 2, C], F32, name="turned")
-            for u in range(2):
-                nc.tensor.transpose(turned[:, u, :], h[e][:].bitcast(F32)[:, u * P : (u + 1) * P], ident[:])
-            nc.scalar.copy(
-                grouped[:, e, :].bitcast(F32).rearrange("p (c u) -> p c u", u=2),
-                turned[:].rearrange("p u c -> p c u"),
-            )
-
+        load_group(0)
+        load_group(1)
         for step in range(E + 1):
-            for g in range(len(SCALE_RUNS)):
-                if step == SCALE_STEP[g]:
+            if step == 2:
+                load_group(2)
+            if step == 4:
+                load_last()
+            for g in range(len(TOKEN_GROUPS)):
+                if step == (0, 1, 3)[g]:
                     gather_scales(g)
-            for e0, e1 in LOAD_RUNS:
-                if step == e0:
-                    gather_words(e0, e1)
             if step < E:
+                gather_words(step)
                 first_layer(step)
             if step >= 1:
-                turn(step - 1)
+                silu(step - 1)
+            for e0, e1 in TURNS:
+                if step == e1:
+                    turn(e0, e1)
 
         for e0, e1 in QUANT_RUNS:
             nc.vector.quantize_mx(

@@ -27,7 +27,7 @@ Y_RUNS = ((0, 4), (4, 7), (7, 8))
 OUT_RUNS = ((0, 384), (384, 512))
 MOVED = 112
 RING = 2
-TOKEN_GROUPS = ((0, 2), (2, 5), (5, 8))
+TOKEN_GROUPS = ((0, 3), (3, 6), (6, 8))
 TURNS = ((0, 2), (2, 4), (4, 6), (6, 7), (7, 8))
 HELD = (1, 3, 5, 6)
 
@@ -99,16 +99,8 @@ def tile_moe_duo_silu_kernel(
             )
         nc.sync.dma_start(out=xw[:], in_=x_words.rearrange("s p t d -> p s (t d)").bitcast(I32))
 
-        def load_group(g):
-            e0, e1 = GROUPS[g]
-            for a in range(2):
-                if g == 0 and a == 0:
-                    load_words(a, e0)
-                    load_planes(a, g)
-                else:
-                    load_planes(a, g)
-                    load_words(a, e0)
-            for e in range(e0 + 1, e1):
+        def load_experts(e0, e1):
+            for e in range(e0, e1):
                 for a in range(2):
                     load_words(a, e)
 
@@ -134,8 +126,7 @@ def tile_moe_duo_silu_kernel(
                 nc.vector.tensor_copy(
                     gathered[g][:, a * width : (a + 1) * width], xs[:].indirect(lists[a][:, e0 * C // 16 : e1 * C // 16])
                 )
-            queue = nc.gpsimd if g == 0 else nc.gpsimd
-            queue.dma_start(
+            nc.sync.dma_start(
                 out=moved[g % RING][0:MOVED, 0 : 2 * width].bitcast(I32), in_=gathered[g][4 : 4 + MOVED, :].bitcast(I32)
             )
             for e in range(e0, e1):
@@ -198,16 +189,31 @@ def tile_moe_duo_silu_kernel(
                 turned[:].rearrange("p e u c -> p e c u"),
             )
 
-        load_group(0)
-        load_group(1)
+        load_words(0, 0)
+        load_planes(0, 0)
+        load_planes(1, 0)
         for step in range(E + 1):
+            if step == 0:
+                gather_scales(0)
+                load_words(1, 0)
+                load_experts(1, 3)
+                load_planes(0, 1)
+                load_words(0, 3)
+            if step == 1:
+                gather_scales(1)
+                load_planes(1, 1)
+                load_words(1, 3)
+                load_experts(4, 6)
             if step == 2:
-                load_group(2)
+                load_planes(0, 2)
+            if step == 3:
+                gather_scales(2)
+                load_words(0, 6)
+                load_planes(1, 2)
+                load_words(1, 6)
+                load_experts(7, 8)
             if step == 4:
                 load_last()
-            for g in range(len(TOKEN_GROUPS)):
-                if step == (0, 1, 3)[g]:
-                    gather_scales(g)
             if step < E:
                 gather_words(step)
                 first_layer(step)

@@ -21,13 +21,15 @@ SILU = mybir.ActivationFunctionType.Silu
 P = 128
 PASSES = K // 512
 SLOTS = E * C
-GROUPS = ((0, 3), (3, 6), (6, 8))
+GROUPS = ((0, 5), (5, 8),)
 QUANT_RUNS = ((0, 4), (4, 6), (6, 7), (7, 8))
 Y_RUNS = ((0, 4), (4, 7), (7, 8))
 OUT_RUNS = ((0, 384), (384, 512))
 MOVED = 112
-RING = 2
-TOKEN_GROUPS = ((0, 3), (3, 6), (6, 8))
+CHUNK = 384
+LOAD_RUNS = ((0, 1), (1, 3), (3, 5), (5, 6), (6, 7), (7, 8),)
+LAP = 0
+TOKEN_GROUPS = ((0, 3), (3, 8),)
 TURNS = ((0, 2), (2, 4), (4, 6), (6, 7), (7, 8))
 HELD = (1, 3, 5, 6)
 
@@ -54,17 +56,19 @@ def tile_moe_duo_silu_kernel(
         back = [keep.tile([P, T // 16], U16, name=f"back_list{a}") for a in range(2)]
         xw = keep.tile([P, PASSES, T], I32, align_bytes=64)
         gathered = [keep.tile([P, 2 * (e1 - e0) * C], U8, name=f"gathered{e0}", align_bytes=64) for e0, e1 in TOKEN_GROUPS]
-        moved = [keep.tile([P, 2 * 3 * C], U8, name=f"moved{g}", align_bytes=64) for g in range(RING)]
+        widths = [2 * (e1 - e0) * C for e0, e1 in TOKEN_GROUPS]
+        moved = keep.tile([P, sum(widths) - (len(widths) - 1) * LAP], U8, name="moved", align_bytes=64)
+        moved_at = [sum(widths[g + 1 :]) - (len(widths) - 1 - g) * LAP for g in range(len(widths))]
         xs = keep.tile([P, T], U8, align_bytes=64)
         planes = [
-            [keep.tile([P, (e1 - e0) * PASSES, H], U8, name=f"plane{a}_{e0}", align_bytes=64) for e0, e1 in GROUPS[:RING]]
+            [keep.tile([P, (e1 - e0) * PASSES, H], U8, name=f"plane{a}_{e0}", align_bytes=64) for e0, e1 in GROUPS]
             for a in range(2)
         ]
         words = [
-            [keep.tile([P, PASSES, 2 * H], U8, name=f"words{a}_{e}", align_bytes=64) for e in range(E)]
+            [keep.tile([P, (e1 - e0) * PASSES, 2 * H], U8, name=f"words{a}_{e0}", align_bytes=64) for e0, e1 in LOAD_RUNS]
             for a in range(2)
         ]
-        w2_plane = planes[0][1][:, 0:PASSES, :].rearrange("p s (q n) -> p (s q) n", n=N)
+        w2_plane = keep.tile([P, E, N], U8, align_bytes=64)
         w2w = keep.tile([P, E, 2 * N], U8, align_bytes=64)
         gates = keep.tile([P, 2, T], F32)
         ident = keep.tile([P, P], F32, align_bytes=64)
@@ -72,24 +76,26 @@ def tile_moe_duo_silu_kernel(
 
         nc.gpsimd.memset(xs[:].bitcast(I32), 0)
         make_identity(nc, ident[:])
-        for g in range(RING):
+        for g in range(len(GROUPS)):
             for a in range(2):
                 nc.vector.memset(planes[a][g][:].bitcast(I32), 0)
-        for g in range(RING):
-            nc.vector.memset(moved[g][:].bitcast(I32), 0)
+            if g == 0:
+                nc.vector.memset(moved[:].bitcast(I32), 0)
+        nc.vector.memset(w2_plane[:].bitcast(I32), 0)
 
         w_words = (w1_words, wp_words)
         w_scales = (w1_scales, wp_scales)
 
-        def load_words(a, e):
+        def load_words(a, c):
+            e0, e1 = LOAD_RUNS[c]
             nc.sync.dma_start(
-                out=words[a][e][:].bitcast(I32),
-                in_=w_words[a][e].rearrange("s p n -> p s n").bitcast(I32),
+                out=words[a][c][:].bitcast(I32),
+                in_=w_words[a][e0:e1].rearrange("e s p n -> p (e s) n").bitcast(I32),
             )
 
         def load_planes(a, g):
             e0, e1 = GROUPS[g]
-            load_scale_rows(nc.sync, planes[a][g % RING][:, 0 : (e1 - e0) * PASSES, :], w_scales[a][e0:e1].rearrange("e s b n -> (e s) b n"))
+            load_scale_rows(nc.sync, planes[a][g], w_scales[a][e0:e1].rearrange("e s b n -> (e s) b n"))
 
         nc.sync.dma_start(lists[0][:], offs)
         nc.sync.dma_start(lists[1][:], offs2)
@@ -123,17 +129,23 @@ def tile_moe_duo_silu_kernel(
             e0, e1 = TOKEN_GROUPS[g]
             width = (e1 - e0) * C
             for a in range(2):
-                nc.vector.tensor_copy(
-                    gathered[g][:, a * width : (a + 1) * width], xs[:].indirect(lists[a][:, e0 * C // 16 : e1 * C // 16])
-                )
-            nc.sync.dma_start(
-                out=moved[g % RING][0:MOVED, 0 : 2 * width].bitcast(I32), in_=gathered[g][4 : 4 + MOVED, :].bitcast(I32)
-            )
+                for j0 in range(0, width, CHUNK):
+                    j1 = min(j0 + CHUNK, width)
+                    nc.vector.tensor_copy(
+                        gathered[g][:, a * width + j0 : a * width + j1],
+                        xs[:].indirect(lists[a][:, (e0 * C + j0) // 16 : (e0 * C + j1) // 16]),
+                    )
             for e in range(e0, e1):
                 for a in range(2):
                     j = a * width + (e - e0) * C
                     tok_planes[a, 0, e] = gathered[g][:, j : j + C]
-                    tok_planes[a, 1, e] = moved[g % RING][:, j : j + C]
+                    tok_planes[a, 1, e] = moved[:, moved_at[g] + j : moved_at[g] + j + C]
+
+        def move_scales(g, queue):
+            queue.dma_start(
+                out=moved[0:MOVED, moved_at[g] : moved_at[g] + widths[g]].bitcast(I32),
+                in_=gathered[g][4 : 4 + MOVED, :].bitcast(I32),
+            )
 
         def gather_words(e):
             for a, s in pass_order(e):
@@ -150,14 +162,15 @@ def tile_moe_duo_silu_kernel(
 
         def first_layer(e):
             g = [e0 <= e < e1 for e0, e1 in GROUPS].index(True)
+            c = [e0 <= e < e1 for e0, e1 in LOAD_RUNS].index(True)
             pre[e] = pre_psum.tile([P, H], F32, name="pre")
             for i, (a, s) in enumerate(pass_order(e)):
                 nc.tensor.matmul_mx(
                     out=pre[e][:],
                     lhsT=tok_words[a, s, e].bitcast(FP8X4),
                     lhsT_scale=tok_planes[a, s, e],
-                    rhs=words[a][e][:, s, :].bitcast(FP4X4),
-                    rhs_scale=planes[a][g % RING][:, (e - GROUPS[g][0]) * PASSES + s, :],
+                    rhs=words[a][c][:, (e - LOAD_RUNS[c][0]) * PASSES + s, :].bitcast(FP4X4),
+                    rhs_scale=planes[a][g][:, (e - GROUPS[g][0]) * PASSES + s, :],
                     start=(i == 0),
                     stop=(i == 2 * PASSES - 1),
                 )
@@ -191,28 +204,27 @@ def tile_moe_duo_silu_kernel(
 
         load_words(0, 0)
         load_planes(0, 0)
+        load_words(1, 0)
         load_planes(1, 0)
         for step in range(E + 1):
             if step == 0:
                 gather_scales(0)
-                load_words(1, 0)
-                load_experts(1, 3)
-                load_planes(0, 1)
-                load_words(0, 3)
+                move_scales(0, nc.sync)
+                load_words(0, 1)
+                load_words(1, 1)
+                load_words(0, 2)
+                load_words(1, 2)
             if step == 1:
                 gather_scales(1)
+                move_scales(1, nc.sync)
+                load_planes(0, 1)
+                load_words(0, 3)
                 load_planes(1, 1)
                 load_words(1, 3)
-                load_experts(4, 6)
-            if step == 2:
-                load_planes(0, 2)
-            if step == 3:
-                gather_scales(2)
-                load_words(0, 6)
-                load_planes(1, 2)
-                load_words(1, 6)
-                load_experts(7, 8)
-            if step == 4:
+                load_words(0, 4)
+                load_words(1, 4)
+                load_words(0, 5)
+                load_words(1, 5)
                 load_last()
             if step < E:
                 gather_words(step)

@@ -28,6 +28,7 @@ OUT_RUNS = ((0, 384), (384, 512))
 MOVED = 112
 CHUNK = 384
 LOAD_RUNS = ((0, 1), (1, 3), (3, 5), (5, 6), (6, 7), (7, 8),)
+GATHER_RUNS = ((0, 1), (1, 3), (3, 5), (5, 7), (7, 8))
 LAP = 0
 TOKEN_GROUPS = ((0, 3), (3, 8),)
 TURNS = ((0, 2), (2, 4), (4, 6), (6, 7), (7, 8))
@@ -68,9 +69,10 @@ def tile_moe_duo_silu_kernel(
             [keep.tile([P, (e1 - e0) * PASSES, 2 * H], U8, name=f"words{a}_{e0}", align_bytes=64) for e0, e1 in LOAD_RUNS]
             for a in range(2)
         ]
-        w2_plane = keep.tile([P, E, N], U8, align_bytes=64)
+        w2_plane = planes[0][0][:, 0:PASSES, :].rearrange("p s (q n) -> p (s q) n", n=N)
         w2w = keep.tile([P, E, 2 * N], U8, align_bytes=64)
         gates = keep.tile([P, 2, T], F32)
+        gate_cols = keep.tile([P, 2, T // P], F32)
         ident = keep.tile([P, P], F32, align_bytes=64)
         y = keep.tile([P, SLOTS], F32)
 
@@ -81,7 +83,6 @@ def tile_moe_duo_silu_kernel(
                 nc.vector.memset(planes[a][g][:].bitcast(I32), 0)
             if g == 0:
                 nc.vector.memset(moved[:].bitcast(I32), 0)
-        nc.vector.memset(w2_plane[:].bitcast(I32), 0)
 
         w_words = (w1_words, wp_words)
         w_scales = (w1_scales, wp_scales)
@@ -99,11 +100,18 @@ def tile_moe_duo_silu_kernel(
 
         nc.sync.dma_start(lists[0][:], offs)
         nc.sync.dma_start(lists[1][:], offs2)
+        nc.sync.dma_start(out=gate_cols[:], in_=gate[:, 0, :].rearrange("r (p c) -> p r c", p=P))
         for q in range(4):
             nc.scalar.dma_start(
                 out=xs[32 * q : 32 * q + 8, :].bitcast(I32), in_=x_scales[:, 4 * q : 4 * q + 4, :].bitcast(I32)
             )
         nc.sync.dma_start(out=xw[:], in_=x_words.rearrange("s p t d -> p s (t d)").bitcast(I32))
+
+        for r in range(2):
+            spread = turn_psum.tile([P, T // P, P], F32, name="turned")
+            for c in range(T // P):
+                nc.tensor.transpose(spread[:, c, :], gate_cols[:, r, c : c + 1].to_broadcast([P, P]), ident[:])
+            nc.scalar.copy(gates[:, r, :].rearrange("m (p c) -> m p c", p=P), spread[:].rearrange("m c p -> m p c"))
 
         def load_experts(e0, e1):
             for e in range(e0, e1):
@@ -115,7 +123,6 @@ def tile_moe_duo_silu_kernel(
             nc.sync.dma_start(out=w2w[:].bitcast(I32), in_=w2_words.rearrange("e s p n -> p (e s) n").bitcast(I32))
             nc.sync.dma_start(back[0][:], pos1)
             nc.sync.dma_start(back[1][:], pos2)
-            nc.sync.dma_start(out=gates[:], in_=gate.rearrange("r p t -> p r t"))
 
         tok_words = {}
         tok_planes = {}
@@ -147,13 +154,16 @@ def tile_moe_duo_silu_kernel(
                 in_=gathered[g][4 : 4 + MOVED, :].bitcast(I32),
             )
 
-        def gather_words(e):
-            for a, s in pass_order(e):
-                tile = keep.tile([P, C], U32, name=f"tok_words{a}_{s}_{e}", tag=f"tok{a}_{s}_{e}", align_bytes=64)
-                nc.vector.tensor_copy(
-                    tile[:], xw[:, s, :].bitcast(U32).indirect(lists[a][:, e * C // 16 : (e + 1) * C // 16])
+        def gather_words(e0, e1):
+            for a, s in pass_order(e0):
+                tile = keep.tile(
+                    [P, (e1 - e0) * C], U32, name=f"tok_words{a}_{s}_{e0}", tag=f"tok{a}_{s}_{e1 - 1}", align_bytes=64
                 )
-                tok_words[a, s, e] = tile[:]
+                nc.vector.tensor_copy(
+                    tile[:], xw[:, s, :].bitcast(U32).indirect(lists[a][:, e0 * C // 16 : e1 * C // 16])
+                )
+                for e in range(e0, e1):
+                    tok_words[a, s, e] = tile[:, (e - e0) * C : (e - e0 + 1) * C]
 
         pre = {}
         grouped = keep.tile([P, E, 4 * C], BF16, align_bytes=64)
@@ -225,9 +235,12 @@ def tile_moe_duo_silu_kernel(
                 load_words(1, 4)
                 load_words(0, 5)
                 load_words(1, 5)
+            if step == GROUPS[0][1]:
                 load_last()
+            for e0, e1 in GATHER_RUNS:
+                if step == e0:
+                    gather_words(e0, e1)
             if step < E:
-                gather_words(step)
                 first_layer(step)
             if step >= 1:
                 silu(step - 1)

@@ -21,18 +21,33 @@ SILU = mybir.ActivationFunctionType.Silu
 P = 128
 PASSES = K // 512
 SLOTS = E * C
-GROUPS = ((0, 5), (5, 8),)
+GROUPS = ((0, 5), (5, 8))
 QUANT_RUNS = ((0, 4), (4, 6), (6, 7), (7, 8))
 Y_RUNS = ((0, 4), (4, 7), (7, 8))
-OUT_RUNS = ((0, 384), (384, 512))
+OUT_RUNS = ((0, 256), (256, 512))
 MOVED = 112
 CHUNK = 384
-LOAD_RUNS = ((0, 1), (1, 3), (3, 5), (5, 6), (6, 7), (7, 8),)
+LOAD_RUNS = ((0, 1), (1, 3), (3, 5), (5, 6), (6, 7), (7, 8))
 GATHER_RUNS = ((0, 1), (1, 3), (3, 5), (5, 7), (7, 8))
 LAP = 0
-TOKEN_GROUPS = ((0, 3), (3, 8),)
+TOKEN_GROUPS = ((0, 3), (3, 8))
 TURNS = ((0, 2), (2, 4), (4, 6), (6, 7), (7, 8))
 HELD = (1, 3, 5, 6)
+XS_WIDTH = 512
+HOLD_ON = {}
+OUT_FORM = 1
+TURN_BANKS = 2
+W2_OWN = 0
+GATE_DIAG = 1
+LAST_AT = 5
+FILL_ORDER = (0, 1)
+WARM = {}
+REUSE = 0
+MOVED_ON_POOL = 0
+MOVE_FORM = 112
+TURN_ON_VECTOR = (6,)
+Y_ON_VECTOR = (0,)
+LOADS = {0: [('gate',), ('xs',), ('x',), ('spread',), ('W', 0, 0), ('P', 0, 0), ('W', 1, 0), ('P', 1, 0), ('S', 0), ('M', 0), ('W', 0, 1), ('W', 1, 1), ('W', 0, 2), ('W', 1, 2)], 1: [('S', 1), ('M', 1), ('P', 0, 1), ('W', 0, 3), ('P', 1, 1), ('W', 1, 3), ('W', 0, 4), ('W', 1, 4), ('W', 0, 5), ('W', 1, 5)]}
 
 
 def load_scale_rows(queue, plane, scales):
@@ -50,8 +65,8 @@ def tile_moe_duo_silu_kernel(
     nc = tc.nc
     with ExitStack() as ctx:
         keep = ctx.enter_context(tc.tile_pool(name="keep", bufs=1))
-        pre_psum = ctx.enter_context(tc.psum_pool(name="pre_psum", bufs=6))
-        turn_psum = ctx.enter_context(tc.psum_pool(name="turn_psum", bufs=2))
+        pre_psum = ctx.enter_context(tc.psum_pool(name="pre_psum", bufs=8 - TURN_BANKS))
+        turn_psum = ctx.enter_context(tc.psum_pool(name="turn_psum", bufs=TURN_BANKS))
 
         lists = [keep.tile([P, SLOTS // 16], U16, name=f"slot_list{a}") for a in range(2)]
         back = [keep.tile([P, T // 16], U16, name=f"back_list{a}") for a in range(2)]
@@ -60,30 +75,47 @@ def tile_moe_duo_silu_kernel(
         widths = [2 * (e1 - e0) * C for e0, e1 in TOKEN_GROUPS]
         moved = keep.tile([P, sum(widths) - (len(widths) - 1) * LAP], U8, name="moved", align_bytes=64)
         moved_at = [sum(widths[g + 1 :]) - (len(widths) - 1 - g) * LAP for g in range(len(widths))]
-        xs = keep.tile([P, T], U8, align_bytes=64)
+        xs = keep.tile([P, XS_WIDTH], U8, align_bytes=64)
         planes = [
-            [keep.tile([P, (e1 - e0) * PASSES, H], U8, name=f"plane{a}_{e0}", align_bytes=64) for e0, e1 in GROUPS]
+            [keep.tile([P, (e1 - e0) * PASSES, H], U8, name=f"plane{a}_{e0}", align_bytes=64) if not (REUSE and e0 > 0) else None for e0, e1 in GROUPS]
             for a in range(2)
         ]
         words = [
-            [keep.tile([P, (e1 - e0) * PASSES, 2 * H], U8, name=f"words{a}_{e0}", align_bytes=64) for e0, e1 in LOAD_RUNS]
+            [keep.tile([P, (e1 - e0) * PASSES, 2 * H], U8, name=f"words{a}_{e0}", align_bytes=64) if not (REUSE and e0 == 0) else None for e0, e1 in LOAD_RUNS]
             for a in range(2)
         ]
+        if REUSE:
+            late = (GROUPS[1][1] - GROUPS[1][0]) * PASSES
+            early = (LOAD_RUNS[0][1] - LOAD_RUNS[0][0]) * PASSES
+            for a in range(2):
+                both = keep.tile([P, max(late, 2 * early) * H], U8, name=f"shared{a}", align_bytes=64)
+                planes[a][1] = both[:, 0 : late * H].rearrange("p (s n) -> p s n", n=H)
+                words[a][0] = both[:, 0 : early * 2 * H].rearrange("p (s n) -> p s n", n=2 * H)
         w2_plane = planes[0][0][:, 0:PASSES, :].rearrange("p s (q n) -> p (s q) n", n=N)
         w2w = keep.tile([P, E, 2 * N], U8, align_bytes=64)
         gates = keep.tile([P, 2, T], F32)
         gate_cols = keep.tile([P, 2, T // P], F32)
+        if W2_OWN:
+            w2_plane = keep.tile([P, E, N], U8, name="w2_plane", align_bytes=64)
         ident = keep.tile([P, P], F32, align_bytes=64)
         y = keep.tile([P, SLOTS], F32)
 
         nc.gpsimd.memset(xs[:].bitcast(I32), 0)
+        if MOVED_ON_POOL:
+            nc.gpsimd.memset(moved[:].bitcast(I32), 0)
         make_identity(nc, ident[:])
-        for g in range(len(GROUPS)):
+        for g in FILL_ORDER:
             for a in range(2):
-                nc.vector.memset(planes[a][g][:].bitcast(I32), 0)
-            if g == 0:
+                if REUSE and g == 1:
+                    if late > 2 * early:
+                        nc.vector.memset(planes[a][g][:, 2 * early :, :].bitcast(I32), 0)
+                else:
+                    nc.vector.memset(planes[a][g][:].bitcast(I32), 0)
+            if g == 0 and not MOVED_ON_POOL:
                 nc.vector.memset(moved[:].bitcast(I32), 0)
 
+        if W2_OWN:
+            nc.vector.memset(w2_plane[:].bitcast(I32), 0)
         w_words = (w1_words, wp_words)
         w_scales = (w1_scales, wp_scales)
 
@@ -94,29 +126,40 @@ def tile_moe_duo_silu_kernel(
                 in_=w_words[a][e0:e1].rearrange("e s p n -> p (e s) n").bitcast(I32),
             )
 
+        def load_pass(a, c, s):
+            e0, e1 = LOAD_RUNS[c]
+            nc.sync.dma_start(out=words[a][c][:, s, :].bitcast(I32), in_=w_words[a][e0, s].bitcast(I32))
+
         def load_planes(a, g):
             e0, e1 = GROUPS[g]
             load_scale_rows(nc.sync, planes[a][g], w_scales[a][e0:e1].rearrange("e s b n -> (e s) b n"))
 
-        nc.sync.dma_start(lists[0][:], offs)
-        nc.sync.dma_start(lists[1][:], offs2)
-        nc.sync.dma_start(out=gate_cols[:], in_=gate[:, 0, :].rearrange("r (p c) -> p r c", p=P))
-        for q in range(4):
-            nc.scalar.dma_start(
-                out=xs[32 * q : 32 * q + 8, :].bitcast(I32), in_=x_scales[:, 4 * q : 4 * q + 4, :].bitcast(I32)
-            )
-        nc.sync.dma_start(out=xw[:], in_=x_words.rearrange("s p t d -> p s (t d)").bitcast(I32))
+        def load_gate():
+            if GATE_DIAG:
+                rows = gate.rearrange("r p (q c) -> (r p q) c", c=8)
+                nc.sync.dma_start(out=gate_cols[:].rearrange("p r c -> p (r c)"), in_=rows[0 : P * P : P + 1, :])
+            else:
+                nc.sync.dma_start(out=gate_cols[:], in_=gate[:, 0, :].rearrange("r (p c) -> p r c", p=P))
 
-        for r in range(2):
-            spread = turn_psum.tile([P, T // P, P], F32, name="turned")
-            for c in range(T // P):
-                nc.tensor.transpose(spread[:, c, :], gate_cols[:, r, c : c + 1].to_broadcast([P, P]), ident[:])
-            nc.scalar.copy(gates[:, r, :].rearrange("m (p c) -> m p c", p=P), spread[:].rearrange("m c p -> m p c"))
+        def load_xs():
+            for q in range(4):
+                nc.scalar.dma_start(
+                    out=xs[32 * q : 32 * q + 8, 0:T].bitcast(I32), in_=x_scales[:, 4 * q : 4 * q + 4, :].bitcast(I32)
+                )
 
-        def load_experts(e0, e1):
-            for e in range(e0, e1):
-                for a in range(2):
-                    load_words(a, e)
+        def load_x():
+            nc.sync.dma_start(out=xw[:], in_=x_words.rearrange("s p t d -> p s (t d)").bitcast(I32))
+
+        def spread_gate():
+            for r in range(2):
+                spread = turn_psum.tile([P, T // P, P], F32, name="turned")
+                for c in range(T // P):
+                    nc.tensor.transpose(spread[:, c, :], gate_cols[:, r, c : c + 1].to_broadcast([P, P]), ident[:])
+                if GATE_DIAG:
+                    target = gates[:].rearrange("m r (p h c) -> m (r p) h c", h=2, c=4)[:, :, r, :]
+                else:
+                    target = gates[:, r, :].rearrange("m (p c) -> m p c", p=P)
+                nc.scalar.copy(target, spread[:].rearrange("m c p -> m p c"))
 
         def load_last():
             load_scale_rows(nc.sync, w2_plane, w2_scales.rearrange("e s b n -> (e s) b n"))
@@ -149,10 +192,27 @@ def tile_moe_duo_silu_kernel(
                     tok_planes[a, 1, e] = moved[:, moved_at[g] + j : moved_at[g] + j + C]
 
         def move_scales(g, queue):
-            queue.dma_start(
-                out=moved[0:MOVED, moved_at[g] : moved_at[g] + widths[g]].bitcast(I32),
-                in_=gathered[g][4 : 4 + MOVED, :].bitcast(I32),
-            )
+            if MOVE_FORM == 112:
+                queue.dma_start(
+                    out=moved[0:MOVED, moved_at[g] : moved_at[g] + widths[g]].bitcast(I32),
+                    in_=gathered[g][4 : 4 + MOVED, :].bitcast(I32),
+                )
+            elif MOVE_FORM == 64:
+                queue.dma_start(
+                    out=moved[0:64, moved_at[g] : moved_at[g] + widths[g]].bitcast(I32),
+                    in_=gathered[g][4:68, :].bitcast(I32),
+                )
+                for q in (64, 96):
+                    queue.dma_start(
+                        out=moved[q : q + 4, moved_at[g] : moved_at[g] + widths[g]].bitcast(I32),
+                        in_=gathered[g][q + 4 : q + 8, :].bitcast(I32),
+                    )
+            else:
+                for r in range(4):
+                    queue.dma_start(
+                        out=moved[r:P:32, moved_at[g] : moved_at[g] + widths[g]].bitcast(I32),
+                        in_=gathered[g][4 + r : P : 32, :].bitcast(I32),
+                    )
 
         def gather_words(e0, e1):
             for a, s in pass_order(e0):
@@ -184,6 +244,18 @@ def tile_moe_duo_silu_kernel(
                     start=(i == 0),
                     stop=(i == 2 * PASSES - 1),
                 )
+                if e == 0 and WARM.get((a, s), 0):
+                    spare = pre_psum.tile([P, H], F32, name="pre")
+                    for j in range(WARM[a, s]):
+                        nc.tensor.matmul_mx(
+                            out=spare[:],
+                            lhsT=tok_words[a, s, e].bitcast(FP8X4),
+                            lhsT_scale=tok_planes[a, s, e],
+                            rhs=words[a][c][:, s, :].bitcast(FP4X4),
+                            rhs_scale=planes[a][g][:, s, :],
+                            start=True,
+                            stop=True,
+                        )
 
         h = {}
 
@@ -191,7 +263,7 @@ def tile_moe_duo_silu_kernel(
             sums = pre[e][:].rearrange("c (p u d) -> c u p d", u=2, d=2)
             if e in HELD or e == E - 1:
                 for u in range(2):
-                    tag = f"tok0_0_{e + 1}" if u == 1 else f"h{e}"
+                    tag = HOLD_ON.get(e, f"tok0_0_{e + 1}") if u == 1 else f"h{e}"
                     half = keep.tile([P, H // 2], BF16, name=f"h{e}_{u}", tag=tag, align_bytes=64)
                     nc.scalar.activation(half[:].rearrange("c (p d) -> c p d", d=2), sums[:, u, :, :], SILU)
                     h[e, u] = half[:].bitcast(F32)
@@ -206,36 +278,35 @@ def tile_moe_duo_silu_kernel(
             order = [(e, u) for e in range(e0, e1) for u in range(2)]
             for e, u in (order if e0 == E - 1 else reversed(order)):
                 nc.tensor.transpose(turned[:, e - e0, u, :], h[e, u], ident[:])
-            copy = nc.vector.tensor_copy if e0 == E - 2 else nc.scalar.copy
+            copy = nc.vector.tensor_copy if e0 in TURN_ON_VECTOR else nc.scalar.copy
             copy(
                 grouped[:, e0:e1, :].bitcast(F32).rearrange("p e (c u) -> p e c u", u=2),
                 turned[:].rearrange("p e u c -> p e c u"),
             )
 
-        load_words(0, 0)
-        load_planes(0, 0)
-        load_words(1, 0)
-        load_planes(1, 0)
+        nc.sync.dma_start(lists[0][:], offs)
+        nc.sync.dma_start(lists[1][:], offs2)
         for step in range(E + 1):
-            if step == 0:
-                gather_scales(0)
-                move_scales(0, nc.sync)
-                load_words(0, 1)
-                load_words(1, 1)
-                load_words(0, 2)
-                load_words(1, 2)
-            if step == 1:
-                gather_scales(1)
-                move_scales(1, nc.sync)
-                load_planes(0, 1)
-                load_words(0, 3)
-                load_planes(1, 1)
-                load_words(1, 3)
-                load_words(0, 4)
-                load_words(1, 4)
-                load_words(0, 5)
-                load_words(1, 5)
-            if step == GROUPS[0][1]:
+            for item in LOADS.get(step, ()):
+                if item[0] == "W":
+                    load_words(item[1], item[2])
+                elif item[0] == "H":
+                    load_pass(item[1], item[2], item[3])
+                elif item[0] == "P":
+                    load_planes(item[1], item[2])
+                elif item[0] == "S":
+                    gather_scales(item[1])
+                elif item[0] == "M":
+                    move_scales(item[1], nc.sync)
+                elif item[0] == "gate":
+                    load_gate()
+                elif item[0] == "spread":
+                    spread_gate()
+                elif item[0] == "xs":
+                    load_xs()
+                elif item[0] == "x":
+                    load_x()
+            if step == LAST_AT:
                 load_last()
             for e0, e1 in GATHER_RUNS:
                 if step == e0:
@@ -266,7 +337,7 @@ def tile_moe_duo_silu_kernel(
                     start=True,
                     stop=True,
                 )
-            if e0 == 0:
+            if e0 in Y_ON_VECTOR:
                 nc.vector.tensor_copy(y[:, e0 * C : e1 * C], acc[:])
             else:
                 nc.scalar.copy(y[:, e0 * C : e1 * C], acc[:])
@@ -283,9 +354,16 @@ def tile_moe_duo_silu_kernel(
             nc.vector.tensor_tensor(result[:, t0:t1], parts[0][:, t0:t1], parts[1][:, t0:t1], ADD)
             nc.sync.dma_start(out=out[:, t0:t1], in_=result[:, t0:t1])
 
-        fetch(0, *OUT_RUNS[0])
-        fetch(1, *OUT_RUNS[0])
-        fetch(0, *OUT_RUNS[1])
-        finish(*OUT_RUNS[0])
-        fetch(1, *OUT_RUNS[1])
-        finish(*OUT_RUNS[1])
+        if OUT_FORM == 0:
+            fetch(0, *OUT_RUNS[0])
+            fetch(1, *OUT_RUNS[0])
+            fetch(0, *OUT_RUNS[1])
+            finish(*OUT_RUNS[0])
+            fetch(1, *OUT_RUNS[1])
+            finish(*OUT_RUNS[1])
+        else:
+            fetch(0, 0, T)
+            for run in OUT_RUNS:
+                fetch(1, *run)
+            for run in OUT_RUNS:
+                finish(*run)

@@ -47,7 +47,7 @@ MOVED_ON_POOL = 0
 MOVE_FORM = 112
 TURN_ON_VECTOR = (6,)
 Y_ON_VECTOR = (0,)
-LOADS = {0: [('gate',), ('xs',), ('x',), ('spread',), ('W', 0, 0), ('P', 0, 0), ('W', 1, 0), ('P', 1, 0), ('S', 0), ('M', 0), ('W', 0, 1), ('W', 1, 1), ('W', 0, 2), ('W', 1, 2)], 1: [('S', 1), ('M', 1), ('P', 0, 1), ('W', 0, 3), ('P', 1, 1), ('W', 1, 3), ('W', 0, 4), ('W', 1, 4), ('W', 0, 5), ('W', 1, 5)]}
+LOADS = {0: [('gate',), ('xs',), ('x',), ('spread',), ('W', 0, 0), ('P', 0, 0), ('W', 1, 0), ('P', 1, 0), ('S', 0), ('M', 0), ('W', 0, 1), ('W', 1, 1), ('W', 0, 2), ('W', 1, 2)], 1: [('S', 1), ('M', 1), ('P', 0, 1), ('P', 1, 1), ('W', 0, 3), ('W', 1, 3), ('W', 0, 4), ('W', 1, 4), ('W', 0, 5), ('W', 1, 5)]}
 
 
 def load_scale_rows(queue, plane, scales):

@@ -22,8 +22,8 @@ P = 128
 PASSES = K // 512
 SLOTS = E * C
 GROUPS = ((0, 5), (5, 8))
-QUANT_RUNS = ((0, 4), (4, 6), (6, 7), (7, 8))
-Y_RUNS = ((0, 4), (4, 7), (7, 8))
+QUANT_RUNS = ((0, 4), (4, 5), (5, 7), (7, 8))
+Y_RUNS = ((0, 4), (4, 5), (5, 7), (7, 8))
 OUT_RUNS = ((0, 256), (256, 512))
 MOVED = 112
 CHUNK = 384
@@ -31,10 +31,12 @@ LOAD_RUNS = ((0, 1), (1, 3), (3, 5), (5, 6), (6, 7), (7, 8))
 GATHER_RUNS = ((0, 1), (1, 3), (3, 5), (5, 7), (7, 8))
 LAP = 0
 TOKEN_GROUPS = ((0, 3), (3, 8))
-TURNS = ((0, 2), (2, 4), (4, 6), (6, 7), (7, 8))
-HELD = (1, 3, 5, 6)
+TURNS = ((0, 2), (2, 4), (4, 5), (5, 7), (7, 8))
+HELD = (1, 3, 6)
 XS_WIDTH = 512
 HOLD_ON = {}
+LATE_LIST = 0
+W2_RUNS = ((0, 4), (4, 8))
 OUT_FORM = 1
 TURN_BANKS = 2
 W2_OWN = 0
@@ -45,8 +47,8 @@ WARM = {}
 REUSE = 0
 MOVED_ON_POOL = 0
 MOVE_FORM = 112
-TURN_ON_VECTOR = (6,)
-Y_ON_VECTOR = (0,)
+TURN_ON_VECTOR = (5,)
+Y_ON_VECTOR = (5,)
 LOADS = {0: [('gate',), ('xs',), ('x',), ('spread',), ('W', 0, 0), ('P', 0, 0), ('W', 1, 0), ('P', 1, 0), ('S', 0), ('M', 0), ('W', 0, 1), ('W', 1, 1), ('W', 0, 2), ('W', 1, 2)], 1: [('S', 1), ('M', 1), ('P', 0, 1), ('P', 1, 1), ('W', 0, 3), ('W', 1, 3), ('W', 0, 4), ('W', 1, 4), ('W', 0, 5), ('W', 1, 5)]}
 
 
@@ -163,7 +165,10 @@ def tile_moe_duo_silu_kernel(
 
         def load_last():
             load_scale_rows(nc.sync, w2_plane, w2_scales.rearrange("e s b n -> (e s) b n"))
-            nc.sync.dma_start(out=w2w[:].bitcast(I32), in_=w2_words.rearrange("e s p n -> p (e s) n").bitcast(I32))
+            for e0, e1 in W2_RUNS:
+                nc.sync.dma_start(
+                    out=w2w[:, e0:e1, :].bitcast(I32), in_=w2_words[e0:e1].rearrange("e s p n -> p (e s) n").bitcast(I32)
+                )
             nc.sync.dma_start(back[0][:], pos1)
             nc.sync.dma_start(back[1][:], pos2)
 
@@ -285,7 +290,8 @@ def tile_moe_duo_silu_kernel(
             )
 
         nc.sync.dma_start(lists[0][:], offs)
-        nc.sync.dma_start(lists[1][:], offs2)
+        if not LATE_LIST:
+            nc.sync.dma_start(lists[1][:], offs2)
         for step in range(E + 1):
             for item in LOADS.get(step, ()):
                 if item[0] == "W":
@@ -302,6 +308,8 @@ def tile_moe_duo_silu_kernel(
                     load_gate()
                 elif item[0] == "spread":
                     spread_gate()
+                elif item[0] == "list":
+                    nc.sync.dma_start(lists[1][:], offs2)
                 elif item[0] == "xs":
                     load_xs()
                 elif item[0] == "x":

@@ -49,7 +49,7 @@ MOVED_ON_POOL = 0
 MOVE_FORM = 112
 TURN_ON_VECTOR = (5,)
 Y_ON_VECTOR = (5,)
-LOADS = {0: [('gate',), ('xs',), ('x',), ('spread',), ('W', 0, 0), ('P', 0, 0), ('W', 1, 0), ('P', 1, 0), ('S', 0), ('M', 0), ('W', 0, 1), ('W', 1, 1), ('W', 0, 2), ('W', 1, 2)], 1: [('S', 1), ('M', 1), ('P', 0, 1), ('P', 1, 1), ('W', 0, 3), ('W', 1, 3), ('W', 0, 4), ('W', 1, 4), ('W', 0, 5), ('W', 1, 5)]}
+LOADS = {0: [('gate',), ('xs',), ('x',), ('spread',), ('W', 0, 0), ('W', 1, 0), ('P', 0, 0), ('P', 1, 0), ('S', 0), ('M', 0), ('W', 0, 1), ('W', 1, 1), ('W', 0, 2), ('W', 1, 2)], 1: [('S', 1), ('M', 1), ('P', 0, 1), ('P', 1, 1), ('W', 0, 3), ('W', 1, 3), ('W', 0, 4), ('W', 1, 4), ('W', 0, 5), ('W', 1, 5)]}
 
 
 def load_scale_rows(queue, plane, scales):

@@ -26,14 +26,14 @@ QUANT_RUNS = ((0, 4), (4, 5), (5, 7), (7, 8))
 Y_RUNS = ((0, 4), (4, 5), (5, 7), (7, 8))
 OUT_RUNS = ((0, 256), (256, 512))
 MOVED = 112
-CHUNK = 384
+CHUNK = 640
 LOAD_RUNS = ((0, 1), (1, 3), (3, 5), (5, 6), (6, 7), (7, 8))
 GATHER_RUNS = ((0, 1), (1, 3), (3, 5), (5, 7), (7, 8))
 LAP = 0
 TOKEN_GROUPS = ((0, 3), (3, 8))
 TURNS = ((0, 2), (2, 4), (4, 5), (5, 7), (7, 8))
 HELD = (1, 3, 6)
-XS_WIDTH = 512
+XS_WIDTH = 896
 HOLD_ON = {}
 LATE_LIST = 0
 W2_RUNS = ((0, 4), (4, 8))
@@ -49,7 +49,7 @@ MOVED_ON_POOL = 0
 MOVE_FORM = 112
 TURN_ON_VECTOR = (5,)
 Y_ON_VECTOR = (5,)
-LOADS = {0: [('gate',), ('xs',), ('x',), ('spread',), ('W', 0, 0), ('W', 1, 0), ('P', 0, 0), ('P', 1, 0), ('S', 0), ('M', 0), ('W', 0, 1), ('W', 1, 1), ('W', 0, 2), ('W', 1, 2)], 1: [('S', 1), ('M', 1), ('P', 0, 1), ('P', 1, 1), ('W', 0, 3), ('W', 1, 3), ('W', 0, 4), ('W', 1, 4), ('W', 0, 5), ('W', 1, 5)]}
+LOADS = {0: [('gate',), ('xs',), ('x',), ('spread',), ('W', 0, 0), ('W', 1, 0), ('P', 0, 0), ('P', 1, 0), ('S', 0), ('M', 0), ('W', 0, 1), ('W', 1, 1), ('W', 0, 2), ('W', 1, 2)], 1: [('G', 0), ('S', 1), ('M', 1), ('G', 1), ('P', 0, 1), ('P', 1, 1), ('W', 0, 3), ('W', 1, 3), ('W', 0, 4), ('W', 1, 4), ('W', 0, 5), ('W', 1, 5)]}
 
 
 def load_scale_rows(queue, plane, scales):
@@ -103,18 +103,12 @@ def tile_moe_duo_silu_kernel(
         y = keep.tile([P, SLOTS], F32)
 
         nc.gpsimd.memset(xs[:].bitcast(I32), 0)
-        if MOVED_ON_POOL:
-            nc.gpsimd.memset(moved[:].bitcast(I32), 0)
+        for a in range(2):
+            nc.vector.memset(planes[a][0][:].bitcast(I32), 0)
+        nc.gpsimd.memset(moved[:].bitcast(I32), 0)
         make_identity(nc, ident[:])
-        for g in FILL_ORDER:
-            for a in range(2):
-                if REUSE and g == 1:
-                    if late > 2 * early:
-                        nc.vector.memset(planes[a][g][:, 2 * early :, :].bitcast(I32), 0)
-                else:
-                    nc.vector.memset(planes[a][g][:].bitcast(I32), 0)
-            if g == 0 and not MOVED_ON_POOL:
-                nc.vector.memset(moved[:].bitcast(I32), 0)
+        for a in range(2):
+            nc.gpsimd.memset(planes[a][1][:].bitcast(I32), 0)
 
         if W2_OWN:
             nc.vector.memset(w2_plane[:].bitcast(I32), 0)
@@ -176,7 +170,7 @@ def tile_moe_duo_silu_kernel(
         tok_planes = {}
 
         def pass_order(e):
-            if e == 0:
+            if e in (0, 3, 4):
                 return [(a, s) for s in range(PASSES) for a in range(2)]
             return [(a, s) for a in range(2) for s in range(PASSES)]
 
@@ -219,8 +213,10 @@ def tile_moe_duo_silu_kernel(
                         in_=gathered[g][4 + r : P : 32, :].bitcast(I32),
                     )
 
-        def gather_words(e0, e1):
+        def gather_words(e0, e1, only=(0, 1)):
             for a, s in pass_order(e0):
+                if a not in only:
+                    continue
                 tile = keep.tile(
                     [P, (e1 - e0) * C], U32, name=f"tok_words{a}_{s}_{e0}", tag=f"tok{a}_{s}_{e1 - 1}", align_bytes=64
                 )
@@ -302,6 +298,8 @@ def tile_moe_duo_silu_kernel(
                     load_planes(item[1], item[2])
                 elif item[0] == "S":
                     gather_scales(item[1])
+                elif item[0] == "G":
+                    gather_words(1, 3, (item[1],))
                 elif item[0] == "M":
                     move_scales(item[1], nc.sync)
                 elif item[0] == "gate":
@@ -317,7 +315,7 @@ def tile_moe_duo_silu_kernel(
             if step == LAST_AT:
                 load_last()
             for e0, e1 in GATHER_RUNS:
-                if step == e0:
+                if step == e0 and step != 1:
                     gather_words(e0, e1)
             if step < E:
                 first_layer(step)

@@ -49,7 +49,7 @@ MOVED_ON_POOL = 0
 MOVE_FORM = 112
 TURN_ON_VECTOR = (5,)
 Y_ON_VECTOR = (5,)
-LOADS = {0: [('gate',), ('xs',), ('x',), ('spread',), ('W', 0, 0), ('W', 1, 0), ('P', 0, 0), ('P', 1, 0), ('S', 0), ('M', 0), ('W', 0, 1), ('W', 1, 1), ('W', 0, 2), ('W', 1, 2)], 1: [('G', 0), ('S', 1), ('M', 1), ('G', 1), ('P', 0, 1), ('P', 1, 1), ('W', 0, 3), ('W', 1, 3), ('W', 0, 4), ('W', 1, 4), ('W', 0, 5), ('W', 1, 5)]}
+LOADS = {0: [('xs',), ('x',), ('W', 1, 0), ('gate',), ('spread',), ('P', 0, 0), ('P', 1, 0), ('S', 0), ('M', 0), ('W', 0, 1), ('W', 1, 1), ('W', 0, 2), ('W', 1, 2)], 1: [('G', 0), ('S', 1), ('M', 1), ('G', 1), ('P', 0, 1), ('P', 1, 1), ('W', 0, 3), ('W', 1, 3), ('W', 0, 4), ('W', 1, 4), ('W', 0, 5), ('W', 1, 5)]}
 
 
 def load_scale_rows(queue, plane, scales):
@@ -285,6 +285,7 @@ def tile_moe_duo_silu_kernel(
                 turned[:].rearrange("p e u c -> p e c u"),
             )
 
+        load_words(0, 0)
         nc.sync.dma_start(lists[0][:], offs)
         if not LATE_LIST:
             nc.sync.dma_start(lists[1][:], offs2)

@@ -21,43 +21,43 @@ SILU = mybir.ActivationFunctionType.Silu
 P = 128
 PASSES = K // 512
 SLOTS = E * C
-GROUPS = ((0, 5), (5, 8))
-QUANT_RUNS = ((0, 4), (4, 5), (5, 7), (7, 8))
-Y_RUNS = ((0, 4), (4, 5), (5, 7), (7, 8))
-OUT_RUNS = ((0, 256), (256, 512))
-MOVED = 112
-CHUNK = 640
-LOAD_RUNS = ((0, 1), (1, 3), (3, 5), (5, 6), (6, 7), (7, 8))
-GATHER_RUNS = ((0, 1), (1, 3), (3, 5), (5, 7), (7, 8))
-LAP = 0
-TOKEN_GROUPS = ((0, 3), (3, 8))
-TURNS = ((0, 2), (2, 4), (4, 5), (5, 7), (7, 8))
-HELD = (1, 3, 6)
-XS_WIDTH = 896
-HOLD_ON = {}
-LATE_LIST = 0
-W2_RUNS = ((0, 4), (4, 8))
-OUT_FORM = 1
+SIDES = (0, 1)
+LAST = E - 1
+
+EARLY = 5
+PLANE_RUNS = ((0, EARLY), (EARLY, E))
+FIRST_BYTES = 3
+BYTE_RUNS = ((0, FIRST_BYTES), (FIRST_BYTES, E))
+PAIRS = tuple((e, e + 2) for e in range(1, EARLY, 2))
+WORD_LOADS = ((0, 1),) + PAIRS + tuple((e, e + 1) for e in range(EARLY, E))
+WORD_GATHERS = ((0, 1),) + tuple((e, e + 2) for e in range(1, LAST, 2)) + ((LAST, E),)
+TURNS = ((0, 2), (2, 4), (EARLY - 1, EARLY), (EARLY, LAST), (LAST, E))
+SECOND_RUNS = ((0, TURNS[1][1]),) + TURNS[2:]
+FIRST_PASSES_FIRST = (0,) + tuple(range(FIRST_BYTES, EARLY))
+SHIFT = 16
+MOVED_ROWS = 112
+WINDOW = 896
 TURN_BANKS = 2
-W2_OWN = 0
-GATE_DIAG = 1
-LAST_AT = 5
-FILL_ORDER = (0, 1)
-WARM = {}
-REUSE = 0
-MOVED_ON_POOL = 0
-MOVE_FORM = 112
-TURN_ON_VECTOR = (5,)
-Y_ON_VECTOR = (5,)
-LOADS = {0: [('xs',), ('x',), ('W', 1, 0), ('gate',), ('spread',), ('P', 0, 0), ('P', 1, 0), ('S', 0), ('M', 0), ('W', 0, 1), ('W', 1, 1), ('W', 0, 2), ('W', 1, 2)], 1: [('G', 0), ('S', 1), ('M', 1), ('G', 1), ('P', 0, 1), ('P', 1, 1), ('W', 0, 3), ('W', 1, 3), ('W', 0, 4), ('W', 1, 4), ('W', 0, 5), ('W', 1, 5)]}
+GATE_PIECE = 8
 
 
-def load_scale_rows(queue, plane, scales):
+def load_scale_rows(nc, plane, scales):
     for r in range(4):
-        queue.dma_start(
+        nc.sync.dma_start(
             out=plane[r:P:32, :, :].bitcast(I32),
-            in_=scales[:, r:16:4, :].rearrange("a q n -> q a n").bitcast(I32),
+            in_=scales[:, r:16:4, :].rearrange("s q n -> q s n").bitcast(I32),
         )
+
+
+def run_of(runs, e):
+    index = [e0 <= e < e1 for e0, e1 in runs].index(True)
+    return index, e - runs[index][0]
+
+
+def pass_order(e):
+    if e in FIRST_PASSES_FIRST:
+        return [(side, s) for s in range(PASSES) for side in SIDES]
+    return [(side, s) for side in SIDES for s in range(PASSES)]
 
 
 def tile_moe_duo_silu_kernel(
@@ -67,310 +67,236 @@ def tile_moe_duo_silu_kernel(
     nc = tc.nc
     with ExitStack() as ctx:
         keep = ctx.enter_context(tc.tile_pool(name="keep", bufs=1))
-        pre_psum = ctx.enter_context(tc.psum_pool(name="pre_psum", bufs=8 - TURN_BANKS))
+        sum_psum = ctx.enter_context(tc.psum_pool(name="sum_psum", bufs=8 - TURN_BANKS))
         turn_psum = ctx.enter_context(tc.psum_pool(name="turn_psum", bufs=TURN_BANKS))
 
-        lists = [keep.tile([P, SLOTS // 16], U16, name=f"slot_list{a}") for a in range(2)]
-        back = [keep.tile([P, T // 16], U16, name=f"back_list{a}") for a in range(2)]
-        xw = keep.tile([P, PASSES, T], I32, align_bytes=64)
-        gathered = [keep.tile([P, 2 * (e1 - e0) * C], U8, name=f"gathered{e0}", align_bytes=64) for e0, e1 in TOKEN_GROUPS]
-        widths = [2 * (e1 - e0) * C for e0, e1 in TOKEN_GROUPS]
-        moved = keep.tile([P, sum(widths) - (len(widths) - 1) * LAP], U8, name="moved", align_bytes=64)
-        moved_at = [sum(widths[g + 1 :]) - (len(widths) - 1 - g) * LAP for g in range(len(widths))]
-        xs = keep.tile([P, XS_WIDTH], U8, align_bytes=64)
-        planes = [
-            [keep.tile([P, (e1 - e0) * PASSES, H], U8, name=f"plane{a}_{e0}", align_bytes=64) if not (REUSE and e0 > 0) else None for e0, e1 in GROUPS]
-            for a in range(2)
+        slot_lists = [keep.tile([P, SLOTS // 16], U16, name=f"slot_list{side}") for side in SIDES]
+        back_lists = [keep.tile([P, T // 16], U16, name=f"back_list{r}") for r in range(2)]
+        word_window = keep.tile([P, PASSES, T], I32, align_bytes=64)
+        byte_widths = [len(SIDES) * (e1 - e0) * C for e0, e1 in BYTE_RUNS]
+        gathered_bytes = [
+            keep.tile([P, width], U8, name=f"gathered_bytes{g}", align_bytes=64) for g, width in enumerate(byte_widths)
         ]
-        words = [
-            [keep.tile([P, (e1 - e0) * PASSES, 2 * H], U8, name=f"words{a}_{e0}", align_bytes=64) if not (REUSE and e0 == 0) else None for e0, e1 in LOAD_RUNS]
-            for a in range(2)
+        moved_bytes = keep.tile([P, sum(byte_widths)], U8, align_bytes=64)
+        moved_at = [byte_widths[1], 0]
+        byte_window = keep.tile([P, WINDOW], U8, align_bytes=64)
+        w_planes = [
+            [
+                keep.tile([P, (e1 - e0) * PASSES, H], U8, name=f"w_plane{side}_{e0}", align_bytes=64)
+                for e0, e1 in PLANE_RUNS
+            ]
+            for side in SIDES
         ]
-        if REUSE:
-            late = (GROUPS[1][1] - GROUPS[1][0]) * PASSES
-            early = (LOAD_RUNS[0][1] - LOAD_RUNS[0][0]) * PASSES
-            for a in range(2):
-                both = keep.tile([P, max(late, 2 * early) * H], U8, name=f"shared{a}", align_bytes=64)
-                planes[a][1] = both[:, 0 : late * H].rearrange("p (s n) -> p s n", n=H)
-                words[a][0] = both[:, 0 : early * 2 * H].rearrange("p (s n) -> p s n", n=2 * H)
-        w2_plane = planes[0][0][:, 0:PASSES, :].rearrange("p s (q n) -> p (s q) n", n=N)
-        w2w = keep.tile([P, E, 2 * N], U8, align_bytes=64)
+        w_words = [
+            [
+                keep.tile([P, (e1 - e0) * PASSES, 2 * H], U8, name=f"w_words{side}_{e0}", align_bytes=64)
+                for e0, e1 in WORD_LOADS
+            ]
+            for side in SIDES
+        ]
+        w2_plane = w_planes[0][0][:, 0:PASSES, :].rearrange("p s (q n) -> p (s q) n", n=N)
+        w2_codes = keep.tile([P, E, 2 * N], U8, align_bytes=64)
         gates = keep.tile([P, 2, T], F32)
-        gate_cols = keep.tile([P, 2, T // P], F32)
-        if W2_OWN:
-            w2_plane = keep.tile([P, E, N], U8, name="w2_plane", align_bytes=64)
+        gate_cols = keep.tile([P, GATE_PIECE], F32)
         ident = keep.tile([P, P], F32, align_bytes=64)
         y = keep.tile([P, SLOTS], F32)
 
-        nc.gpsimd.memset(xs[:].bitcast(I32), 0)
-        for a in range(2):
-            nc.vector.memset(planes[a][0][:].bitcast(I32), 0)
-        nc.gpsimd.memset(moved[:].bitcast(I32), 0)
+        nc.gpsimd.memset(byte_window[:].bitcast(I32), 0)
+        for side in SIDES:
+            nc.vector.memset(w_planes[side][0][:].bitcast(I32), 0)
+        nc.gpsimd.memset(moved_bytes[:].bitcast(I32), 0)
         make_identity(nc, ident[:])
-        for a in range(2):
-            nc.gpsimd.memset(planes[a][1][:].bitcast(I32), 0)
+        for side in SIDES:
+            nc.gpsimd.memset(w_planes[side][1][:].bitcast(I32), 0)
 
-        if W2_OWN:
-            nc.vector.memset(w2_plane[:].bitcast(I32), 0)
-        w_words = (w1_words, wp_words)
-        w_scales = (w1_scales, wp_scales)
+        words_in = (w1_words, wp_words)
+        scales_in = (w1_scales, wp_scales)
 
-        def load_words(a, c):
-            e0, e1 = LOAD_RUNS[c]
+        def load_words(side, c):
+            e0, e1 = WORD_LOADS[c]
             nc.sync.dma_start(
-                out=words[a][c][:].bitcast(I32),
-                in_=w_words[a][e0:e1].rearrange("e s p n -> p (e s) n").bitcast(I32),
+                out=w_words[side][c][:].bitcast(I32),
+                in_=words_in[side][e0:e1].rearrange("e s p n -> p (e s) n").bitcast(I32),
             )
 
-        def load_pass(a, c, s):
-            e0, e1 = LOAD_RUNS[c]
-            nc.sync.dma_start(out=words[a][c][:, s, :].bitcast(I32), in_=w_words[a][e0, s].bitcast(I32))
+        def load_planes(g):
+            e0, e1 = PLANE_RUNS[g]
+            for side in SIDES:
+                load_scale_rows(nc, w_planes[side][g], scales_in[side][e0:e1].rearrange("e s b n -> (e s) b n"))
 
-        def load_planes(a, g):
-            e0, e1 = GROUPS[g]
-            load_scale_rows(nc.sync, planes[a][g], w_scales[a][e0:e1].rearrange("e s b n -> (e s) b n"))
-
-        def load_gate():
-            if GATE_DIAG:
-                rows = gate.rearrange("r p (q c) -> (r p q) c", c=8)
-                nc.sync.dma_start(out=gate_cols[:].rearrange("p r c -> p (r c)"), in_=rows[0 : P * P : P + 1, :])
-            else:
-                nc.sync.dma_start(out=gate_cols[:], in_=gate[:, 0, :].rearrange("r (p c) -> p r c", p=P))
-
-        def load_xs():
-            for q in range(4):
+        def load_token_scales():
+            for r in range(4):
                 nc.scalar.dma_start(
-                    out=xs[32 * q : 32 * q + 8, 0:T].bitcast(I32), in_=x_scales[:, 4 * q : 4 * q + 4, :].bitcast(I32)
+                    out=byte_window[r:P:SHIFT, 0:T].bitcast(I32),
+                    in_=x_scales[:, r:16:4, :].rearrange("s q t -> q s t").bitcast(I32),
                 )
 
-        def load_x():
-            nc.sync.dma_start(out=xw[:], in_=x_words.rearrange("s p t d -> p s (t d)").bitcast(I32))
-
-        def spread_gate():
-            for r in range(2):
-                spread = turn_psum.tile([P, T // P, P], F32, name="turned")
-                for c in range(T // P):
-                    nc.tensor.transpose(spread[:, c, :], gate_cols[:, r, c : c + 1].to_broadcast([P, P]), ident[:])
-                if GATE_DIAG:
-                    target = gates[:].rearrange("m r (p h c) -> m (r p) h c", h=2, c=4)[:, :, r, :]
-                else:
-                    target = gates[:, r, :].rearrange("m (p c) -> m p c", p=P)
+        def load_and_spread_gate():
+            pieces = gate.rearrange("r p (q c) -> (r p q) c", c=GATE_PIECE)
+            nc.sync.dma_start(out=gate_cols[:], in_=pieces[0 : P * P : P + 1, :])
+            for half in range(2):
+                spread = turn_psum.tile([P, GATE_PIECE // 2, P], F32, name="turned")
+                for c in range(GATE_PIECE // 2):
+                    column = half * (GATE_PIECE // 2) + c
+                    nc.tensor.transpose(spread[:, c, :], gate_cols[:, column : column + 1].to_broadcast([P, P]), ident[:])
+                target = gates[:].rearrange("m r (p h c) -> m (r p) h c", h=2, c=GATE_PIECE // 2)[:, :, half, :]
                 nc.scalar.copy(target, spread[:].rearrange("m c p -> m p c"))
 
-        def load_last():
-            load_scale_rows(nc.sync, w2_plane, w2_scales.rearrange("e s b n -> (e s) b n"))
-            for e0, e1 in W2_RUNS:
+        def load_second_layer():
+            load_scale_rows(nc, w2_plane, w2_scales.rearrange("e s b n -> (e s) b n"))
+            for e0 in range(0, E, E // 2):
                 nc.sync.dma_start(
-                    out=w2w[:, e0:e1, :].bitcast(I32), in_=w2_words[e0:e1].rearrange("e s p n -> p (e s) n").bitcast(I32)
+                    out=w2_codes[:, e0 : e0 + E // 2, :].bitcast(I32),
+                    in_=w2_words[e0 : e0 + E // 2].rearrange("e s p n -> p (e s) n").bitcast(I32),
                 )
-            nc.sync.dma_start(back[0][:], pos1)
-            nc.sync.dma_start(back[1][:], pos2)
+            nc.sync.dma_start(back_lists[0][:], pos1)
+            nc.sync.dma_start(back_lists[1][:], pos2)
 
-        tok_words = {}
-        tok_planes = {}
+        slot_words = {}
+        slot_planes = {}
 
-        def pass_order(e):
-            if e in (0, 3, 4):
-                return [(a, s) for s in range(PASSES) for a in range(2)]
-            return [(a, s) for a in range(2) for s in range(PASSES)]
-
-        def gather_scales(g):
-            e0, e1 = TOKEN_GROUPS[g]
+        def gather_and_move_bytes(g):
+            e0, e1 = BYTE_RUNS[g]
             width = (e1 - e0) * C
-            for a in range(2):
-                for j0 in range(0, width, CHUNK):
-                    j1 = min(j0 + CHUNK, width)
-                    nc.vector.tensor_copy(
-                        gathered[g][:, a * width + j0 : a * width + j1],
-                        xs[:].indirect(lists[a][:, (e0 * C + j0) // 16 : (e0 * C + j1) // 16]),
-                    )
-            for e in range(e0, e1):
-                for a in range(2):
-                    j = a * width + (e - e0) * C
-                    tok_planes[a, 0, e] = gathered[g][:, j : j + C]
-                    tok_planes[a, 1, e] = moved[:, moved_at[g] + j : moved_at[g] + j + C]
-
-        def move_scales(g, queue):
-            if MOVE_FORM == 112:
-                queue.dma_start(
-                    out=moved[0:MOVED, moved_at[g] : moved_at[g] + widths[g]].bitcast(I32),
-                    in_=gathered[g][4 : 4 + MOVED, :].bitcast(I32),
-                )
-            elif MOVE_FORM == 64:
-                queue.dma_start(
-                    out=moved[0:64, moved_at[g] : moved_at[g] + widths[g]].bitcast(I32),
-                    in_=gathered[g][4:68, :].bitcast(I32),
-                )
-                for q in (64, 96):
-                    queue.dma_start(
-                        out=moved[q : q + 4, moved_at[g] : moved_at[g] + widths[g]].bitcast(I32),
-                        in_=gathered[g][q + 4 : q + 8, :].bitcast(I32),
-                    )
-            else:
-                for r in range(4):
-                    queue.dma_start(
-                        out=moved[r:P:32, moved_at[g] : moved_at[g] + widths[g]].bitcast(I32),
-                        in_=gathered[g][4 + r : P : 32, :].bitcast(I32),
-                    )
-
-        def gather_words(e0, e1, only=(0, 1)):
-            for a, s in pass_order(e0):
-                if a not in only:
-                    continue
-                tile = keep.tile(
-                    [P, (e1 - e0) * C], U32, name=f"tok_words{a}_{s}_{e0}", tag=f"tok{a}_{s}_{e1 - 1}", align_bytes=64
-                )
+            for side in SIDES:
                 nc.vector.tensor_copy(
-                    tile[:], xw[:, s, :].bitcast(U32).indirect(lists[a][:, e0 * C // 16 : e1 * C // 16])
+                    gathered_bytes[g][:, side * width : (side + 1) * width],
+                    byte_window[:].indirect(slot_lists[side][:, e0 * C // 16 : e1 * C // 16]),
                 )
-                for e in range(e0, e1):
-                    tok_words[a, s, e] = tile[:, (e - e0) * C : (e - e0 + 1) * C]
+            for e in range(e0, e1):
+                for side in SIDES:
+                    j = side * width + (e - e0) * C
+                    slot_planes[side, 0, e] = gathered_bytes[g][:, j : j + C]
+                    slot_planes[side, 1, e] = moved_bytes[:, moved_at[g] + j : moved_at[g] + j + C]
+            nc.sync.dma_start(
+                out=moved_bytes[0:MOVED_ROWS, moved_at[g] : moved_at[g] + byte_widths[g]].bitcast(I32),
+                in_=gathered_bytes[g][SHIFT : SHIFT + MOVED_ROWS, :].bitcast(I32),
+            )
 
-        pre = {}
-        grouped = keep.tile([P, E, 4 * C], BF16, align_bytes=64)
+        def gather_words(e0, e1, sides):
+            for side, s in pass_order(e0):
+                if side in sides:
+                    tile = keep.tile([P, (e1 - e0) * C], U32, name=f"slot_words{side}_{s}_{e1 - 1}", align_bytes=64)
+                    nc.vector.tensor_copy(
+                        tile[:],
+                        word_window[:, s, :].bitcast(U32).indirect(slot_lists[side][:, e0 * C // 16 : e1 * C // 16]),
+                    )
+                    for e in range(e0, e1):
+                        slot_words[side, s, e] = tile[:, (e - e0) * C : (e - e0 + 1) * C]
+
+        sums = {}
+        h_turned = keep.tile([P, E, 4 * C], BF16, align_bytes=64)
         h_words = keep.tile([P, SLOTS], U32, align_bytes=64)
-        h_scales = keep.tile([P, SLOTS], U8, align_bytes=64)
+        h_plane = keep.tile([P, SLOTS], U8, align_bytes=64)
 
         def first_layer(e):
-            g = [e0 <= e < e1 for e0, e1 in GROUPS].index(True)
-            c = [e0 <= e < e1 for e0, e1 in LOAD_RUNS].index(True)
-            pre[e] = pre_psum.tile([P, H], F32, name="pre")
-            for i, (a, s) in enumerate(pass_order(e)):
+            g, in_planes = run_of(PLANE_RUNS, e)
+            c, in_words = run_of(WORD_LOADS, e)
+            sums[e] = sum_psum.tile([P, H], F32, name="sums")
+            for index, (side, s) in enumerate(pass_order(e)):
                 nc.tensor.matmul_mx(
-                    out=pre[e][:],
-                    lhsT=tok_words[a, s, e].bitcast(FP8X4),
-                    lhsT_scale=tok_planes[a, s, e],
-                    rhs=words[a][c][:, (e - LOAD_RUNS[c][0]) * PASSES + s, :].bitcast(FP4X4),
-                    rhs_scale=planes[a][g][:, (e - GROUPS[g][0]) * PASSES + s, :],
-                    start=(i == 0),
-                    stop=(i == 2 * PASSES - 1),
+                    out=sums[e][:],
+                    lhsT=slot_words[side, s, e].bitcast(FP8X4),
+                    lhsT_scale=slot_planes[side, s, e],
+                    rhs=w_words[side][c][:, in_words * PASSES + s, :].bitcast(FP4X4),
+                    rhs_scale=w_planes[side][g][:, in_planes * PASSES + s, :],
+                    start=(index == 0),
+                    stop=(index == len(SIDES) * PASSES - 1),
                 )
-                if e == 0 and WARM.get((a, s), 0):
-                    spare = pre_psum.tile([P, H], F32, name="pre")
-                    for j in range(WARM[a, s]):
-                        nc.tensor.matmul_mx(
-                            out=spare[:],
-                            lhsT=tok_words[a, s, e].bitcast(FP8X4),
-                            lhsT_scale=tok_planes[a, s, e],
-                            rhs=words[a][c][:, s, :].bitcast(FP4X4),
-                            rhs_scale=planes[a][g][:, s, :],
-                            start=True,
-                            stop=True,
-                        )
 
-        h = {}
+        h_pairs = {}
+        pair_ends = [e1 - 1 for e0, e1 in TURNS if e1 - e0 == 2]
 
         def silu(e):
-            sums = pre[e][:].rearrange("c (p u d) -> c u p d", u=2, d=2)
-            if e in HELD or e == E - 1:
+            by_pair = sums[e][:].rearrange("c (p u d) -> c u p d", u=2, d=2)
+            if e in pair_ends or e == LAST:
                 for u in range(2):
-                    tag = HOLD_ON.get(e, f"tok0_0_{e + 1}") if u == 1 else f"h{e}"
+                    tag = f"slot_words0_0_{e + 1}" if u == 1 and e != LAST else f"h{e}_{u}"
                     half = keep.tile([P, H // 2], BF16, name=f"h{e}_{u}", tag=tag, align_bytes=64)
-                    nc.scalar.activation(half[:].rearrange("c (p d) -> c p d", d=2), sums[:, u, :, :], SILU)
-                    h[e, u] = half[:].bitcast(F32)
+                    nc.scalar.activation(half[:].rearrange("c (p d) -> c p d", d=2), by_pair[:, u, :, :], SILU)
+                    h_pairs[e, u] = half[:].bitcast(F32)
             else:
                 both = keep.tile([P, H], BF16, name=f"h{e}", align_bytes=64)
-                nc.scalar.activation(both[:].rearrange("c (u p d) -> c u p d", u=2, d=2), sums, SILU)
+                nc.scalar.activation(both[:].rearrange("c (u p d) -> c u p d", u=2, d=2), by_pair, SILU)
                 for u in range(2):
-                    h[e, u] = both[:].bitcast(F32)[:, u * P : (u + 1) * P]
+                    h_pairs[e, u] = both[:].bitcast(F32)[:, u * P : (u + 1) * P]
 
         def turn(e0, e1):
             turned = turn_psum.tile([P, e1 - e0, 2, C], F32, name="turned")
             order = [(e, u) for e in range(e0, e1) for u in range(2)]
-            for e, u in (order if e0 == E - 1 else reversed(order)):
-                nc.tensor.transpose(turned[:, e - e0, u, :], h[e, u], ident[:])
-            copy = nc.vector.tensor_copy if e0 in TURN_ON_VECTOR else nc.scalar.copy
+            for e, u in order if e0 == LAST else reversed(order):
+                nc.tensor.transpose(turned[:, e - e0, u, :], h_pairs[e, u], ident[:])
+            copy = nc.vector.tensor_copy if e0 == EARLY else nc.scalar.copy
             copy(
-                grouped[:, e0:e1, :].bitcast(F32).rearrange("p e (c u) -> p e c u", u=2),
+                h_turned[:, e0:e1, :].bitcast(F32).rearrange("p e (c u) -> p e c u", u=2),
                 turned[:].rearrange("p e u c -> p e c u"),
             )
 
+        nc.sync.dma_start(slot_lists[0][:], offs)
         load_words(0, 0)
-        nc.sync.dma_start(lists[0][:], offs)
-        if not LATE_LIST:
-            nc.sync.dma_start(lists[1][:], offs2)
-        for step in range(E + 1):
-            for item in LOADS.get(step, ()):
-                if item[0] == "W":
-                    load_words(item[1], item[2])
-                elif item[0] == "H":
-                    load_pass(item[1], item[2], item[3])
-                elif item[0] == "P":
-                    load_planes(item[1], item[2])
-                elif item[0] == "S":
-                    gather_scales(item[1])
-                elif item[0] == "G":
-                    gather_words(1, 3, (item[1],))
-                elif item[0] == "M":
-                    move_scales(item[1], nc.sync)
-                elif item[0] == "gate":
-                    load_gate()
-                elif item[0] == "spread":
-                    spread_gate()
-                elif item[0] == "list":
-                    nc.sync.dma_start(lists[1][:], offs2)
-                elif item[0] == "xs":
-                    load_xs()
-                elif item[0] == "x":
-                    load_x()
-            if step == LAST_AT:
-                load_last()
-            for e0, e1 in GATHER_RUNS:
-                if step == e0 and step != 1:
-                    gather_words(e0, e1)
+        nc.sync.dma_start(slot_lists[1][:], offs2)
+        load_token_scales()
+        nc.sync.dma_start(out=word_window[:], in_=x_words.rearrange("s p t d -> p s (t d)").bitcast(I32))
+        load_words(1, 0)
+        load_and_spread_gate()
+        load_planes(0)
+        gather_and_move_bytes(0)
+        for c in range(1, 1 + len(PAIRS)):
+            for side in SIDES:
+                load_words(side, c)
+        gather_words(*WORD_GATHERS[0], SIDES)
+        first_layer(0)
+
+        gather_words(*WORD_GATHERS[1], SIDES[:1])
+        gather_and_move_bytes(1)
+        gather_words(*WORD_GATHERS[1], SIDES[1:])
+        load_planes(1)
+        for c in range(1 + len(PAIRS), len(WORD_LOADS)):
+            for side in SIDES:
+                load_words(side, c)
+
+        for step in range(1, E + 1):
+            if step == EARLY:
+                load_second_layer()
+            for e0, e1 in WORD_GATHERS[2:]:
+                if step == e0:
+                    gather_words(e0, e1, SIDES)
             if step < E:
                 first_layer(step)
-            if step >= 1:
-                silu(step - 1)
+            silu(step - 1)
             for e0, e1 in TURNS:
                 if step == e1:
                     turn(e0, e1)
 
-        for e0, e1 in QUANT_RUNS:
+        for e0, e1 in SECOND_RUNS:
             nc.vector.quantize_mx(
                 out=h_words[:, e0 * C : e1 * C].bitcast(FP8X4),
-                scales=h_scales[:, e0 * C : e1 * C],
-                in_=grouped[:, e0:e1, :].rearrange("p e c -> p (e c)"),
+                scales=h_plane[:, e0 * C : e1 * C],
+                in_=h_turned[:, e0:e1, :].rearrange("p e c -> p (e c)"),
             )
-        for e0, e1 in Y_RUNS:
-            acc = pre_psum.tile([P, (e1 - e0) * C], F32, name="pre")
+        for e0, e1 in SECOND_RUNS:
+            y_bank = sum_psum.tile([P, (e1 - e0) * C], F32, name="sums")
             for e in range(e0, e1):
                 nc.tensor.matmul_mx(
-                    out=acc[:, (e - e0) * C : (e - e0 + 1) * C],
-                    lhsT=w2w[:, e, :].bitcast(FP4X4),
+                    out=y_bank[:, (e - e0) * C : (e - e0 + 1) * C],
+                    lhsT=w2_codes[:, e, :].bitcast(FP4X4),
                     lhsT_scale=w2_plane[:, e, :],
                     rhs=h_words[:, e * C : (e + 1) * C].bitcast(FP8X4),
-                    rhs_scale=h_scales[:, e * C : (e + 1) * C],
+                    rhs_scale=h_plane[:, e * C : (e + 1) * C],
                     start=True,
                     stop=True,
                 )
-            if e0 in Y_ON_VECTOR:
-                nc.vector.tensor_copy(y[:, e0 * C : e1 * C], acc[:])
-            else:
-                nc.scalar.copy(y[:, e0 * C : e1 * C], acc[:])
+            copy = nc.vector.tensor_copy if e0 == EARLY else nc.scalar.copy
+            copy(y[:, e0 * C : e1 * C], y_bank[:])
 
         parts = [keep.tile([P, T], F32, name=f"part{r}") for r in range(2)]
         result = keep.tile([P, T], F32)
-
-        def fetch(r, t0, t1):
-            nc.vector.tensor_tensor(
-                parts[r][:, t0:t1], y[:].indirect(back[r][:, t0 // 16 : t1 // 16]), gates[:, r, t0:t1], MULT
-            )
-
-        def finish(t0, t1):
+        halves = ((0, T // 2), (T // 2, T))
+        for r, runs in enumerate((((0, T),), halves)):
+            for t0, t1 in runs:
+                nc.vector.tensor_tensor(
+                    parts[r][:, t0:t1], y[:].indirect(back_lists[r][:, t0 // 16 : t1 // 16]), gates[:, r, t0:t1], MULT
+                )
+        for t0, t1 in halves:
             nc.vector.tensor_tensor(result[:, t0:t1], parts[0][:, t0:t1], parts[1][:, t0:t1], ADD)
             nc.sync.dma_start(out=out[:, t0:t1], in_=result[:, t0:t1])
-
-        if OUT_FORM == 0:
-            fetch(0, *OUT_RUNS[0])
-            fetch(1, *OUT_RUNS[0])
-            fetch(0, *OUT_RUNS[1])
-            finish(*OUT_RUNS[0])
-            fetch(1, *OUT_RUNS[1])
-            finish(*OUT_RUNS[1])
-        else:
-            fetch(0, 0, T)
-            for run in OUT_RUNS:
-                fetch(1, *run)
-            for run in OUT_RUNS:
-                finish(*run)

@@ -17,6 +17,7 @@ FP4X4 = mybir.dt.float4_e2m1fn_x4
 MULT = mybir.AluOpType.mult
 ADD = mybir.AluOpType.add
 SILU = mybir.ActivationFunctionType.Silu
+COPY = mybir.ActivationFunctionType.Copy
 
 P = 128
 PASSES = K // 512
@@ -289,14 +290,20 @@ def tile_moe_duo_silu_kernel(
             copy = nc.vector.tensor_copy if e0 == EARLY else nc.scalar.copy
             copy(y[:, e0 * C : e1 * C], y_bank[:])
 
-        parts = [keep.tile([P, T], F32, name=f"part{r}") for r in range(2)]
+        half = T // 2
+        fetched = {}
+        for r, t0 in ((1, 0), (1, half)):
+            fetched[r, t0] = keep.tile([P, half], F32, name=f"fetched{r}_{t0}")
+            nc.scalar.activation(fetched[r, t0][:], y[:].indirect(back_lists[r][:, t0 // 16 : (t0 + half) // 16]), COPY)
+        parts = {(r, t0): keep.tile([P, half], F32, name=f"part{r}_{t0}") for r in range(2) for t0 in (0, half)}
         result = keep.tile([P, T], F32)
-        halves = ((0, T // 2), (T // 2, T))
-        for r, runs in enumerate((((0, T),), halves)):
-            for t0, t1 in runs:
-                nc.vector.tensor_tensor(
-                    parts[r][:, t0:t1], y[:].indirect(back_lists[r][:, t0 // 16 : t1 // 16]), gates[:, r, t0:t1], MULT
-                )
-        for t0, t1 in halves:
-            nc.vector.tensor_tensor(result[:, t0:t1], parts[0][:, t0:t1], parts[1][:, t0:t1], ADD)
-            nc.sync.dma_start(out=out[:, t0:t1], in_=result[:, t0:t1])
+        for t0 in (0, half):
+            nc.vector.tensor_tensor(
+                parts[0, t0][:], y[:].indirect(back_lists[0][:, t0 // 16 : (t0 + half) // 16]), gates[:, 0, t0 : t0 + half], MULT
+            )
+        for t0 in (0, half):
+            for r in (1, 0):
+                if (r, t0) in fetched:
+                    nc.vector.tensor_tensor(parts[r, t0][:], fetched[r, t0][:], gates[:, r, t0 : t0 + half], MULT)
+            nc.vector.tensor_tensor(result[:, t0 : t0 + half], parts[0, t0][:], parts[1, t0][:], ADD)
+            nc.sync.dma_start(out=out[:, t0 : t0 + half], in_=result[:, t0 : t0 + half])

@@ -95,7 +95,7 @@ def tile_moe_duo_silu_kernel(
             ]
             for side in SIDES
         ]
-        w2_plane = w_planes[0][0][:, 0:PASSES, :].rearrange("p s (q n) -> p (s q) n", n=N)
+        w2_plane = keep.tile([P, E, N], U8, align_bytes=64)
         w2_codes = keep.tile([P, E, 2 * N], U8, align_bytes=64)
         gates = keep.tile([P, 2, T], F32)
         gate_cols = keep.tile([P, GATE_PIECE], F32)
@@ -103,12 +103,7 @@ def tile_moe_duo_silu_kernel(
         y = keep.tile([P, SLOTS], F32)
 
         nc.gpsimd.memset(byte_window[:].bitcast(I32), 0)
-        for side in SIDES:
-            nc.vector.memset(w_planes[side][0][:].bitcast(I32), 0)
-        nc.gpsimd.memset(moved_bytes[:].bitcast(I32), 0)
         make_identity(nc, ident[:])
-        for side in SIDES:
-            nc.gpsimd.memset(w_planes[side][1][:].bitcast(I32), 0)
 
         words_in = (w1_words, wp_words)
         scales_in = (w1_scales, wp_scales)

@@ -73,7 +73,7 @@ def tile_moe_duo_silu_kernel(
 
         slot_lists = [keep.tile([P, SLOTS // 16], U16, name=f"slot_list{side}") for side in SIDES]
         back_lists = [keep.tile([P, T // 16], U16, name=f"back_list{r}") for r in range(2)]
-        word_window = keep.tile([P, PASSES, T], I32, align_bytes=64)
+        word_window = keep.tile([P, PASSES, T], I32, align_bytes=256)
         byte_widths = [len(SIDES) * (e1 - e0) * C for e0, e1 in BYTE_RUNS]
         gathered_bytes = [
             keep.tile([P, width], U8, name=f"gathered_bytes{g}", align_bytes=64) for g, width in enumerate(byte_widths)
@@ -83,14 +83,14 @@ def tile_moe_duo_silu_kernel(
         byte_window = keep.tile([P, WINDOW], U8, align_bytes=64)
         w_planes = [
             [
-                keep.tile([P, (e1 - e0) * PASSES, H], U8, name=f"w_plane{side}_{e0}", align_bytes=64)
+                keep.tile([P, (e1 - e0) * PASSES, H], U8, name=f"w_plane{side}_{e0}", align_bytes=256)
                 for e0, e1 in PLANE_RUNS
             ]
             for side in SIDES
         ]
         w_words = [
             [
-                keep.tile([P, (e1 - e0) * PASSES, 2 * H], U8, name=f"w_words{side}_{e0}", align_bytes=64)
+                keep.tile([P, (e1 - e0) * PASSES, 2 * H], U8, name=f"w_words{side}_{e0}", align_bytes=256)
                 for e0, e1 in WORD_LOADS
             ]
             for side in SIDES
@@ -139,12 +139,8 @@ def tile_moe_duo_silu_kernel(
                 nc.scalar.copy(target, spread[:].rearrange("m c p -> m p c"))
 
         def load_second_layer():
+            nc.sync.dma_start(out=w2_codes[:].bitcast(I32), in_=w2_words.rearrange("e s p n -> p (e s) n").bitcast(I32))
             load_scale_rows(nc, w2_plane, w2_scales.rearrange("e s b n -> (e s) b n"))
-            for e0 in range(0, E, E // 2):
-                nc.sync.dma_start(
-                    out=w2_codes[:, e0 : e0 + E // 2, :].bitcast(I32),
-                    in_=w2_words[e0 : e0 + E // 2].rearrange("e s p n -> p (e s) n").bitcast(I32),
-                )
             nc.sync.dma_start(back_lists[0][:], pos1)
             nc.sync.dma_start(back_lists[1][:], pos2)
 
@@ -291,7 +287,7 @@ def tile_moe_duo_silu_kernel(
             fetched[r, t0] = keep.tile([P, half], F32, name=f"fetched{r}_{t0}")
             nc.scalar.activation(fetched[r, t0][:], y[:].indirect(back_lists[r][:, t0 // 16 : (t0 + half) // 16]), COPY)
         parts = {(r, t0): keep.tile([P, half], F32, name=f"part{r}_{t0}") for r in range(2) for t0 in (0, half)}
-        result = keep.tile([P, T], F32)
+        result = keep.tile([P, T], F32, align_bytes=256)
         for t0 in (0, half):
             nc.vector.tensor_tensor(
                 parts[0, t0][:], y[:].indirect(back_lists[0][:, t0 // 16 : (t0 + half) // 16]), gates[:, 0, t0 : t0 + half], MULT

@@ -36,10 +36,11 @@ TURNS = ((0, 2), (2, 4), (EARLY - 1, EARLY), (EARLY, LAST), (LAST, E))
 SECOND_RUNS = ((0, TURNS[1][1]),) + TURNS[2:]
 FIRST_PASSES_FIRST = (0,) + tuple(range(FIRST_BYTES, EARLY))
 SHIFT = 16
-MOVED_ROWS = 112
+MOVED_ROWS = 3 * 32 + 4
 WINDOW = 896
 TURN_BANKS = 2
 GATE_PIECE = 8
+ALIGN = 256
 
 
 def load_scale_rows(nc, plane, scales):
@@ -73,33 +74,33 @@ def tile_moe_duo_silu_kernel(
 
         slot_lists = [keep.tile([P, SLOTS // 16], U16, name=f"slot_list{side}") for side in SIDES]
         back_lists = [keep.tile([P, T // 16], U16, name=f"back_list{r}") for r in range(2)]
-        word_window = keep.tile([P, PASSES, T], I32, align_bytes=256)
+        word_window = keep.tile([P, PASSES, T], I32, align_bytes=ALIGN)
         byte_widths = [len(SIDES) * (e1 - e0) * C for e0, e1 in BYTE_RUNS]
         gathered_bytes = [
-            keep.tile([P, width], U8, name=f"gathered_bytes{g}", align_bytes=64) for g, width in enumerate(byte_widths)
+            keep.tile([P, width], U8, name=f"gathered_bytes{g}", align_bytes=ALIGN) for g, width in enumerate(byte_widths)
         ]
-        moved_bytes = keep.tile([P, sum(byte_widths)], U8, align_bytes=64)
+        moved_bytes = keep.tile([P, sum(byte_widths)], U8, align_bytes=ALIGN)
         moved_at = [byte_widths[1], 0]
-        byte_window = keep.tile([P, WINDOW], U8, align_bytes=64)
+        byte_window = keep.tile([P, WINDOW], U8, align_bytes=ALIGN)
         w_planes = [
             [
-                keep.tile([P, (e1 - e0) * PASSES, H], U8, name=f"w_plane{side}_{e0}", align_bytes=256)
+                keep.tile([P, (e1 - e0) * PASSES, H], U8, name=f"w_plane{side}_{e0}", align_bytes=ALIGN)
                 for e0, e1 in PLANE_RUNS
             ]
             for side in SIDES
         ]
         w_words = [
             [
-                keep.tile([P, (e1 - e0) * PASSES, 2 * H], U8, name=f"w_words{side}_{e0}", align_bytes=256)
+                keep.tile([P, (e1 - e0) * PASSES, 2 * H], U8, name=f"w_words{side}_{e0}", align_bytes=ALIGN)
                 for e0, e1 in WORD_LOADS
             ]
             for side in SIDES
         ]
-        w2_plane = keep.tile([P, E, N], U8, align_bytes=64)
-        w2_codes = keep.tile([P, E, 2 * N], U8, align_bytes=64)
+        w2_plane = keep.tile([P, E, N], U8, align_bytes=ALIGN)
+        w2_codes = keep.tile([P, E, 2 * N], U8, align_bytes=ALIGN)
         gates = keep.tile([P, 2, T], F32)
         gate_cols = keep.tile([P, GATE_PIECE], F32)
-        ident = keep.tile([P, P], F32, align_bytes=64)
+        ident = keep.tile([P, P], F32, align_bytes=ALIGN)
         y = keep.tile([P, SLOTS], F32)
 
         nc.gpsimd.memset(byte_window[:].bitcast(I32), 0)
@@ -168,7 +169,7 @@ def tile_moe_duo_silu_kernel(
         def gather_words(e0, e1, sides):
             for side, s in pass_order(e0):
                 if side in sides:
-                    tile = keep.tile([P, (e1 - e0) * C], U32, name=f"slot_words{side}_{s}_{e1 - 1}", align_bytes=64)
+                    tile = keep.tile([P, (e1 - e0) * C], U32, name=f"slot_words{side}_{s}_{e1 - 1}", align_bytes=ALIGN)
                     nc.vector.tensor_copy(
                         tile[:],
                         word_window[:, s, :].bitcast(U32).indirect(slot_lists[side][:, e0 * C // 16 : e1 * C // 16]),
@@ -177,9 +178,9 @@ def tile_moe_duo_silu_kernel(
                         slot_words[side, s, e] = tile[:, (e - e0) * C : (e - e0 + 1) * C]
 
         sums = {}
-        h_turned = keep.tile([P, E, 4 * C], BF16, align_bytes=64)
-        h_words = keep.tile([P, SLOTS], U32, align_bytes=64)
-        h_plane = keep.tile([P, SLOTS], U8, align_bytes=64)
+        h_turned = keep.tile([P, E, 4 * C], BF16, align_bytes=ALIGN)
+        h_words = keep.tile([P, SLOTS], U32, align_bytes=ALIGN)
+        h_plane = keep.tile([P, SLOTS], U8, align_bytes=ALIGN)
 
         def first_layer(e):
             g, in_planes = run_of(PLANE_RUNS, e)
@@ -204,11 +205,11 @@ def tile_moe_duo_silu_kernel(
             if e in pair_ends or e == LAST:
                 for u in range(2):
                     tag = f"slot_words0_0_{e + 1}" if u == 1 and e != LAST else f"h{e}_{u}"
-                    half = keep.tile([P, H // 2], BF16, name=f"h{e}_{u}", tag=tag, align_bytes=64)
+                    half = keep.tile([P, H // 2], BF16, name=f"h{e}_{u}", tag=tag, align_bytes=ALIGN)
                     nc.scalar.activation(half[:].rearrange("c (p d) -> c p d", d=2), by_pair[:, u, :, :], SILU)
                     h_pairs[e, u] = half[:].bitcast(F32)
             else:
-                both = keep.tile([P, H], BF16, name=f"h{e}", align_bytes=64)
+                both = keep.tile([P, H], BF16, name=f"h{e}", align_bytes=ALIGN)
                 nc.scalar.activation(both[:].rearrange("c (u p d) -> c u p d", u=2, d=2), by_pair, SILU)
                 for u in range(2):
                     h_pairs[e, u] = both[:].bitcast(F32)[:, u * P : (u + 1) * P]
@@ -281,20 +282,20 @@ def tile_moe_duo_silu_kernel(
             copy = nc.vector.tensor_copy if e0 == EARLY else nc.scalar.copy
             copy(y[:, e0 * C : e1 * C], y_bank[:])
 
-        half = T // 2
-        fetched = {}
-        for r, t0 in ((1, 0), (1, half)):
-            fetched[r, t0] = keep.tile([P, half], F32, name=f"fetched{r}_{t0}")
-            nc.scalar.activation(fetched[r, t0][:], y[:].indirect(back_lists[r][:, t0 // 16 : (t0 + half) // 16]), COPY)
-        parts = {(r, t0): keep.tile([P, half], F32, name=f"part{r}_{t0}") for r in range(2) for t0 in (0, half)}
-        result = keep.tile([P, T], F32, align_bytes=256)
-        for t0 in (0, half):
-            nc.vector.tensor_tensor(
-                parts[0, t0][:], y[:].indirect(back_lists[0][:, t0 // 16 : (t0 + half) // 16]), gates[:, 0, t0 : t0 + half], MULT
-            )
-        for t0 in (0, half):
-            for r in (1, 0):
-                if (r, t0) in fetched:
-                    nc.vector.tensor_tensor(parts[r, t0][:], fetched[r, t0][:], gates[:, r, t0 : t0 + half], MULT)
-            nc.vector.tensor_tensor(result[:, t0 : t0 + half], parts[0, t0][:], parts[1, t0][:], ADD)
-            nc.sync.dma_start(out=out[:, t0 : t0 + half], in_=result[:, t0 : t0 + half])
+        width = T // 2
+        starts = (0, width)
+
+        def slots_of(r, t0):
+            return y[:].indirect(back_lists[r][:, t0 // 16 : (t0 + width) // 16])
+
+        fetched = {t0: keep.tile([P, width], F32, name=f"fetched{t0}") for t0 in starts}
+        for t0 in starts:
+            nc.scalar.activation(fetched[t0][:], slots_of(1, t0), COPY)
+        parts = {(r, t0): keep.tile([P, width], F32, name=f"part{r}_{t0}") for r in range(2) for t0 in starts}
+        result = keep.tile([P, T], F32, align_bytes=ALIGN)
+        for t0 in starts:
+            nc.vector.tensor_tensor(parts[0, t0][:], slots_of(0, t0), gates[:, 0, t0 : t0 + width], MULT)
+        for t0 in starts:
+            nc.vector.tensor_tensor(parts[1, t0][:], fetched[t0][:], gates[:, 1, t0 : t0 + width], MULT)
+            nc.vector.tensor_tensor(result[:, t0 : t0 + width], parts[0, t0][:], parts[1, t0][:], ADD)
+            nc.sync.dma_start(out=out[:, t0 : t0 + width], in_=result[:, t0 : t0 + width])

from contextlib import ExitStack

import concourse.mybir as mybir
from concourse.masks import make_identity

K, T, E, C, H, N = 1024, 512, 8, 128, 512, 128
FLOPS = 2 * E * C * (2 * K * H + H * N)

F32 = mybir.dt.float32
BF16 = mybir.dt.bfloat16
I32 = mybir.dt.int32
U32 = mybir.dt.uint32
U16 = mybir.dt.uint16
U8 = mybir.dt.uint8
FP8X4 = mybir.dt.float8_e4m3fn_x4
FP4X4 = mybir.dt.float4_e2m1fn_x4
MULT = mybir.AluOpType.mult
ADD = mybir.AluOpType.add
SILU = mybir.ActivationFunctionType.Silu
COPY = mybir.ActivationFunctionType.Copy

P = 128
PASSES = K // 512
SLOTS = E * C
SIDES = (0, 1)
LAST = E - 1

EARLY = 5
PLANE_RUNS = ((0, EARLY), (EARLY, E))
FIRST_BYTES = 3
BYTE_RUNS = ((0, FIRST_BYTES), (FIRST_BYTES, E))
PAIRS = tuple((e, e + 2) for e in range(1, EARLY, 2))
WORD_LOADS = ((0, 1),) + PAIRS + tuple((e, e + 1) for e in range(EARLY, E))
WORD_GATHERS = ((0, 1),) + tuple((e, e + 2) for e in range(1, LAST, 2)) + ((LAST, E),)
TURNS = ((0, 2), (2, 4), (EARLY - 1, EARLY), (EARLY, LAST), (LAST, E))
SECOND_RUNS = ((0, TURNS[1][1]),) + TURNS[2:]
FIRST_PASSES_FIRST = (0,) + tuple(range(FIRST_BYTES, EARLY))
SHIFT = 16
MOVED_ROWS = 3 * 32 + 4
WINDOW = 896
TURN_BANKS = 2
GATE_PIECE = 8
ALIGN = 256


def load_scale_rows(nc, plane, scales):
    for r in range(4):
        nc.sync.dma_start(
            out=plane[r:P:32, :, :].bitcast(I32),
            in_=scales[:, r:16:4, :].rearrange("s q n -> q s n").bitcast(I32),
        )


def run_of(runs, e):
    index = [e0 <= e < e1 for e0, e1 in runs].index(True)
    return index, e - runs[index][0]


def pass_order(e):
    if e in FIRST_PASSES_FIRST:
        return [(side, s) for s in range(PASSES) for side in SIDES]
    return [(side, s) for side in SIDES for s in range(PASSES)]


def tile_moe_duo_silu_kernel(
    tc, x_words, x_scales, w1_words, w1_scales, wp_words, wp_scales, w2_words, w2_scales,
    gate, offs, pos1, pos2, offs2, out,
):
    nc = tc.nc
    with ExitStack() as ctx:
        keep = ctx.enter_context(tc.tile_pool(name="keep", bufs=1))
        sum_psum = ctx.enter_context(tc.psum_pool(name="sum_psum", bufs=8 - TURN_BANKS))
        turn_psum = ctx.enter_context(tc.psum_pool(name="turn_psum", bufs=TURN_BANKS))

        slot_lists = [keep.tile([P, SLOTS // 16], U16, name=f"slot_list{side}") for side in SIDES]
        back_lists = [keep.tile([P, T // 16], U16, name=f"back_list{r}") for r in range(2)]
        word_window = keep.tile([P, PASSES, T], I32, align_bytes=ALIGN)
        byte_widths = [len(SIDES) * (e1 - e0) * C for e0, e1 in BYTE_RUNS]
        gathered_bytes = [
            keep.tile([P, width], U8, name=f"gathered_bytes{g}", align_bytes=ALIGN) for g, width in enumerate(byte_widths)
        ]
        moved_bytes = keep.tile([P, sum(byte_widths)], U8, align_bytes=ALIGN)
        moved_at = [byte_widths[1], 0]
        byte_window = keep.tile([P, WINDOW], U8, align_bytes=ALIGN)
        w_planes = [
            [
                keep.tile([P, (e1 - e0) * PASSES, H], U8, name=f"w_plane{side}_{e0}", align_bytes=ALIGN)
                for e0, e1 in PLANE_RUNS
            ]
            for side in SIDES
        ]
        w_words = [
            [
                keep.tile([P, (e1 - e0) * PASSES, 2 * H], U8, name=f"w_words{side}_{e0}", align_bytes=ALIGN)
                for e0, e1 in WORD_LOADS
            ]
            for side in SIDES
        ]
        w2_plane = keep.tile([P, E, N], U8, align_bytes=ALIGN)
        w2_codes = keep.tile([P, E, 2 * N], U8, align_bytes=ALIGN)
        gates = keep.tile([P, 2, T], F32)
        gate_cols = keep.tile([P, GATE_PIECE], F32)
        ident = keep.tile([P, P], F32, align_bytes=ALIGN)
        y = keep.tile([P, SLOTS], F32)

        nc.gpsimd.memset(byte_window[:].bitcast(I32), 0)
        make_identity(nc, ident[:])

        words_in = (w1_words, wp_words)
        scales_in = (w1_scales, wp_scales)

        def load_words(side, c):
            e0, e1 = WORD_LOADS[c]
            nc.sync.dma_start(
                out=w_words[side][c][:].bitcast(I32),
                in_=words_in[side][e0:e1].rearrange("e s p n -> p (e s) n").bitcast(I32),
            )

        def load_planes(g):
            e0, e1 = PLANE_RUNS[g]
            for side in SIDES:
                load_scale_rows(nc, w_planes[side][g], scales_in[side][e0:e1].rearrange("e s b n -> (e s) b n"))

        def load_token_scales():
            for r in range(4):
                nc.scalar.dma_start(
                    out=byte_window[r:P:SHIFT, 0:T].bitcast(I32),
                    in_=x_scales[:, r:16:4, :].rearrange("s q t -> q s t").bitcast(I32),
                )

        def load_and_spread_gate():
            pieces = gate.rearrange("r p (q c) -> (r p q) c", c=GATE_PIECE)
            nc.sync.dma_start(out=gate_cols[:], in_=pieces[0 : P * P : P + 1, :])
            for half in range(2):
                spread = turn_psum.tile([P, GATE_PIECE // 2, P], F32, name="turned")
                for c in range(GATE_PIECE // 2):
                    column = half * (GATE_PIECE // 2) + c
                    nc.tensor.transpose(spread[:, c, :], gate_cols[:, column : column + 1].to_broadcast([P, P]), ident[:])
                target = gates[:].rearrange("m r (p h c) -> m (r p) h c", h=2, c=GATE_PIECE // 2)[:, :, half, :]
                nc.scalar.copy(target, spread[:].rearrange("m c p -> m p c"))

        def load_second_layer():
            nc.sync.dma_start(out=w2_codes[:].bitcast(I32), in_=w2_words.rearrange("e s p n -> p (e s) n").bitcast(I32))
            load_scale_rows(nc, w2_plane, w2_scales.rearrange("e s b n -> (e s) b n"))
            nc.sync.dma_start(back_lists[0][:], pos1)
            nc.sync.dma_start(back_lists[1][:], pos2)

        slot_words = {}
        slot_planes = {}

        def gather_and_move_bytes(g):
            e0, e1 = BYTE_RUNS[g]
            width = (e1 - e0) * C
            for side in SIDES:
                nc.vector.tensor_copy(
                    gathered_bytes[g][:, side * width : (side + 1) * width],
                    byte_window[:].indirect(slot_lists[side][:, e0 * C // 16 : e1 * C // 16]),
                )
            for e in range(e0, e1):
                for side in SIDES:
                    j = side * width + (e - e0) * C
                    slot_planes[side, 0, e] = gathered_bytes[g][:, j : j + C]
                    slot_planes[side, 1, e] = moved_bytes[:, moved_at[g] + j : moved_at[g] + j + C]
            nc.sync.dma_start(
                out=moved_bytes[0:MOVED_ROWS, moved_at[g] : moved_at[g] + byte_widths[g]].bitcast(I32),
                in_=gathered_bytes[g][SHIFT : SHIFT + MOVED_ROWS, :].bitcast(I32),
            )

        def gather_words(e0, e1, sides):
            for side, s in pass_order(e0):
                if side in sides:
                    tile = keep.tile([P, (e1 - e0) * C], U32, name=f"slot_words{side}_{s}_{e1 - 1}", align_bytes=ALIGN)
                    nc.vector.tensor_copy(
                        tile[:],
                        word_window[:, s, :].bitcast(U32).indirect(slot_lists[side][:, e0 * C // 16 : e1 * C // 16]),
                    )
                    for e in range(e0, e1):
                        slot_words[side, s, e] = tile[:, (e - e0) * C : (e - e0 + 1) * C]

        sums = {}
        h_turned = keep.tile([P, E, 4 * C], BF16, align_bytes=ALIGN)
        h_words = keep.tile([P, SLOTS], U32, align_bytes=ALIGN)
        h_plane = keep.tile([P, SLOTS], U8, align_bytes=ALIGN)

        def first_layer(e):
            g, in_planes = run_of(PLANE_RUNS, e)
            c, in_words = run_of(WORD_LOADS, e)
            sums[e] = sum_psum.tile([P, H], F32, name="sums")
            for index, (side, s) in enumerate(pass_order(e)):
                nc.tensor.matmul_mx(
                    out=sums[e][:],
                    lhsT=slot_words[side, s, e].bitcast(FP8X4),
                    lhsT_scale=slot_planes[side, s, e],
                    rhs=w_words[side][c][:, in_words * PASSES + s, :].bitcast(FP4X4),
                    rhs_scale=w_planes[side][g][:, in_planes * PASSES + s, :],
                    start=(index == 0),
                    stop=(index == len(SIDES) * PASSES - 1),
                )

        h_pairs = {}
        pair_ends = [e1 - 1 for e0, e1 in TURNS if e1 - e0 == 2]

        def silu(e):
            by_pair = sums[e][:].rearrange("c (p u d) -> c u p d", u=2, d=2)
            if e in pair_ends or e == LAST:
                for u in range(2):
                    tag = f"slot_words0_0_{e + 1}" if u == 1 and e != LAST else f"h{e}_{u}"
                    half = keep.tile([P, H // 2], BF16, name=f"h{e}_{u}", tag=tag, align_bytes=ALIGN)
                    nc.scalar.activation(half[:].rearrange("c (p d) -> c p d", d=2), by_pair[:, u, :, :], SILU)
                    h_pairs[e, u] = half[:].bitcast(F32)
            else:
                both = keep.tile([P, H], BF16, name=f"h{e}", align_bytes=ALIGN)
                nc.scalar.activation(both[:].rearrange("c (u p d) -> c u p d", u=2, d=2), by_pair, SILU)
                for u in range(2):
                    h_pairs[e, u] = both[:].bitcast(F32)[:, u * P : (u + 1) * P]

        def turn(e0, e1):
            turned = turn_psum.tile([P, e1 - e0, 2, C], F32, name="turned")
            order = [(e, u) for e in range(e0, e1) for u in range(2)]
            for e, u in order if e0 == LAST else reversed(order):
                nc.tensor.transpose(turned[:, e - e0, u, :], h_pairs[e, u], ident[:])
            copy = nc.vector.tensor_copy if e0 == EARLY else nc.scalar.copy
            copy(
                h_turned[:, e0:e1, :].bitcast(F32).rearrange("p e (c u) -> p e c u", u=2),
                turned[:].rearrange("p e u c -> p e c u"),
            )

        nc.sync.dma_start(slot_lists[0][:], offs)
        load_words(0, 0)
        nc.sync.dma_start(slot_lists[1][:], offs2)
        load_token_scales()
        nc.sync.dma_start(out=word_window[:], in_=x_words.rearrange("s p t d -> p s (t d)").bitcast(I32))
        load_words(1, 0)
        load_and_spread_gate()
        load_planes(0)
        gather_and_move_bytes(0)
        for c in range(1, 1 + len(PAIRS)):
            for side in SIDES:
                load_words(side, c)
        gather_words(*WORD_GATHERS[0], SIDES)
        first_layer(0)

        gather_words(*WORD_GATHERS[1], SIDES[:1])
        gather_and_move_bytes(1)
        gather_words(*WORD_GATHERS[1], SIDES[1:])
        load_planes(1)
        for c in range(1 + len(PAIRS), len(WORD_LOADS)):
            for side in SIDES:
                load_words(side, c)

        for step in range(1, E + 1):
            if step == EARLY:
                load_second_layer()
            for e0, e1 in WORD_GATHERS[2:]:
                if step == e0:
                    gather_words(e0, e1, SIDES)
            if step < E:
                first_layer(step)
            silu(step - 1)
            for e0, e1 in TURNS:
                if step == e1:
                    turn(e0, e1)

        for e0, e1 in SECOND_RUNS:
            nc.vector.quantize_mx(
                out=h_words[:, e0 * C : e1 * C].bitcast(FP8X4),
                scales=h_plane[:, e0 * C : e1 * C],
                in_=h_turned[:, e0:e1, :].rearrange("p e c -> p (e c)"),
            )
        for e0, e1 in SECOND_RUNS:
            y_bank = sum_psum.tile([P, (e1 - e0) * C], F32, name="sums")
            for e in range(e0, e1):
                nc.tensor.matmul_mx(
                    out=y_bank[:, (e - e0) * C : (e - e0 + 1) * C],
                    lhsT=w2_codes[:, e, :].bitcast(FP4X4),
                    lhsT_scale=w2_plane[:, e, :],
                    rhs=h_words[:, e * C : (e + 1) * C].bitcast(FP8X4),
                    rhs_scale=h_plane[:, e * C : (e + 1) * C],
                    start=True,
                    stop=True,
                )
            copy = nc.vector.tensor_copy if e0 == EARLY else nc.scalar.copy
            copy(y[:, e0 * C : e1 * C], y_bank[:])

        width = T // 2
        starts = (0, width)

        def slots_of(r, t0):
            return y[:].indirect(back_lists[r][:, t0 // 16 : (t0 + width) // 16])

        fetched = {t0: keep.tile([P, width], F32, name=f"fetched{t0}") for t0 in starts}
        for t0 in starts:
            nc.scalar.activation(fetched[t0][:], slots_of(1, t0), COPY)
        parts = {(r, t0): keep.tile([P, width], F32, name=f"part{r}_{t0}") for r in range(2) for t0 in starts}
        result = keep.tile([P, T], F32, align_bytes=ALIGN)
        for t0 in starts:
            nc.vector.tensor_tensor(parts[0, t0][:], slots_of(0, t0), gates[:, 0, t0 : t0 + width], MULT)
        for t0 in starts:
            nc.vector.tensor_tensor(parts[1, t0][:], fetched[t0][:], gates[:, 1, t0 : t0 + width], MULT)
            nc.vector.tensor_tensor(result[:, t0 : t0 + width], parts[0, t0][:], parts[1, t0][:], ADD)
            nc.sync.dma_start(out=out[:, t0 : t0 + width], in_=result[:, t0 : t0 + width])
